import numpy as np, ml_dtypes
CORES = [16,17,18,19,32,33,34,35]
N = 8
BF = ml_dtypes.bfloat16
def gentries(a):
    return np.ascontiguousarray(a.reshape(8, 16, -1).transpose(0, 2, 1)).reshape(8, -1)
def gtable(e):
    e = np.asarray(e); return np.ascontiguousarray(e.reshape(8, -1, 16).transpose(0, 2, 1)).reshape(128, -1).astype(np.int32)
T, C, E, D = 2048, 2048, 128, 4
def ints(rng, *shape):
    return rng.integers(-15, 16, shape).astype(np.float32).astype(BF)
def uneven(rng, *shape):
    s = rng.choice(np.array([0, 1, 3, 7, 15, 15]), shape[:-2] + (1, shape[-1]))
    return ((rng.integers(-15, 16, shape) * s) // 15).astype(np.float32).astype(BF)
def trees(rng, out, alone, tight, across):
    H = T // 2; i = np.arange(T); r = np.arange(N)[:, None, None]
    back = np.where(rng.random((N, 8, T)) < 0.5, rng.integers(1, 9, (N, 8, T)), 1 + np.floor(i * rng.random((N, 8, T))).astype(np.int64))
    pa = np.maximum(i - back, 0)
    pa = np.where(rng.random((N, 8, T)) < alone, i, pa)
    pa = np.where((rng.random((N, 8, T)) < out) & (i >= H) & (r > 0), T + rng.integers(0, E, (N, 8, T)), pa)
    at = rng.integers(0, H, (N, 8, E))
    if tight:
        w = H + np.arange(tight * D).reshape(tight, D)
        pa[:, :, w[:, :-1].reshape(-1)] = w[:, 1:].reshape(-1)
        pa[:, :, w[:, -1]] = np.where(r > 0, T + rng.integers(0, E, (N, 8, tight)), rng.integers(0, H, (N, 8, tight)))
        at[:, :, :tight] = w[:, 0]
    at = rng.permuted(at, axis=2)
    num = rng.permuted(np.tile(i, (N, 8, 1)), axis=2)
    par = np.zeros((N, 8, T), np.int64)
    np.put_along_axis(par, num, np.where(pa < T, np.take_along_axis(num, np.minimum(pa, T - 1), 2), pa), 2)
    ex = np.take_along_axis(np.roll(num, 1, axis=0), at, 2)
    u = np.where(rng.random((N, 8, C)) < 0.75, rng.integers(H, T, (N, 8, C)), rng.integers(0, T, (N, 8, C)))
    up = np.take_along_axis(num, u, 2)
    up = np.where((rng.random((N, 8, C)) < across) & (r > 0), T + rng.integers(0, E, (N, 8, C)), up)
    return up, par, ex
def pack(rng, up, par, ex):
    ex = ex.copy(); ex[0] = rng.integers(0, T, (8, E))
    return {"q": ints(rng, N, 128, C), "k": ints(rng, N, 128, T), "v": ints(rng, N, 128, T), "b": rng.integers(-15, 16, (N, 128, D)).astype(np.float32),
            "up": np.stack([gtable(a) for a in up]), "par": par.astype(np.int32), "ex": np.stack([gtable(a) for a in ex])}
def setup_inputs(rng):
    return pack(rng, *trees(rng, 0.125, 0.015625, E // 4, 0.125))
def setup_inputs_roots(rng):
    up, par, ex = trees(rng, 0.125, 0.5, 0, 0.125)
    par[:, :, 0] = 0; par[:, :, T - 1] = T - 1; par[:, :, 1] = 2; par[:, :, 2] = 3; par[:, :, 3] = 1
    ex[:, :, 0] = 0; ex[:, :, E - 1] = T - 1; ex[:, :, 1] = 1
    up[:, :, 0] = 0; up[:, :, 1] = T - 1; up[:, :, 2] = 1
    up[1:, :, 3] = T; up[1:, :, 4] = T + 1; up[1:, :, C - 1] = T + E - 1; up[0, :, C - 1] = T - 1
    return pack(rng, up, par, ex)
def setup_inputs_brink(rng):
    return pack(rng, *trees(rng, 0.5, 0.015625, E, 0.5))
def setup_inputs_alike(rng):
    up, par, ex = trees(rng, 0.25, 0.015625, 0, 0.0)
    up = np.repeat(up[:, :, :1], C, axis=2); ex = np.repeat(ex[:, :, :1], E, axis=2)
    up[rng.integers(1, N)] = T + rng.integers(0, E, (8, 1))
    return pack(rng, up, par, ex)
def setup_inputs_spread(rng):
    d = setup_inputs(rng)
    d["q"] = uneven(rng, N, 128, C); d["k"] = uneven(rng, N, 128, T); d["v"] = uneven(rng, N, 128, T)
    d["b"] = rng.choice(np.array([-15, -1, 0, 0, 1, 15]), (N, 128, D)).astype(np.float32); return d
def check_inputs(d):
    bad = []
    for n in ("q", "k", "v", "b"):
        w = d[n].astype(np.float32)
        if not ((np.abs(w) <= 15) & (w == np.rint(w))).all(): bad.append(n + ": whole numbers from -15 to 15")
    for n in ("up", "par"):
        w = d[n]
        if w.min() < 0 or w.max() >= T + E or w[0].max() >= T: bad.append(n + ": range")
    if d["ex"].min() < 0 or d["ex"].max() >= T: bad.append("ex: range")
    if bad: return bad
    for r in range(1, N):
        a = gentries(d["ex"][r]).astype(np.int64)
        for t in range(D - 1):
            a = np.take_along_axis(d["par"][r - 1], a, 1).astype(np.int64)
            if (a >= T).any(): return ["the nodes above an exit's node"]
    return bad
def reference(q, k, v, b, up, par, ex):
    y = np.zeros((N, 128, C), np.float32)
    u = np.stack([gentries(a) for a in up]).astype(np.int64); x = np.stack([gentries(a) for a in ex]).astype(np.int64)
    def place(m, r, g):
        return np.where(m < T, r * T + m, (r - 1) * T + x[r, g][np.maximum(m - T, 0)])
    for g in range(8):
        s = slice(16 * g, 16 * g + 16)
        above = np.concatenate([place(par[r, g].astype(np.int64), r, g) for r in range(N)])
        kk = np.concatenate([k[r, s].astype(np.float32) for r in range(N)], axis=1); vv = np.concatenate([v[r, s].astype(np.float32) for r in range(N)], axis=1)
        for r in range(N):
            a = place(u[r, g], r, g); qq = q[r, s].astype(np.float32)
            for t in range(D):
                y[r, s] += np.maximum(qq - kk[:, a] + b[r, s, t:t + 1], np.float32(0)) * vv[:, a]
                a = above[a]
    return {"y": y}

@@ -1,0 +1,307 @@
+from concourse.bass import DstId, RemoteDMATransfer
+from concourse.mybir import AluOpType, ActivationFunctionType
+
+ALU = AluOpType
+ACT = ActivationFunctionType
+NT, NE, ND = 2048, 128, 4
+BIG = float(2 ** 50)
+TINY = 1.0 / BIG
+
+UNITS = [(1, 0, 1024, "a"), (2, 0, 1024, "d"), (3, 0, 1024, "a"), (4, 0, 1024, "d"), (1, 1024, 2048, "d"),
+         (2, 1024, 2048, "a"), (3, 1024, 2048, "d"), (4, 1024, 1536, "a"), (4, 1536, 2048, "a")]
+FINALS = [(0, 512, "S"), (512, 1024, "S"), (1024, 1536, "S"), (1536, 1792, "V"), (1792, 2048, "V")]
+SENDS = [[0], [1], [2, 3]]
+NENG = 8
+QAFTER = {"lqa": "sx", "lqb": "sd0"}
+ORDER = {
+    "V": "z0 k1 ca cl cf cw z1 k2 cm cb z2 e0 e2 ix ih in ib d1 xu d2 up d3 w1 w4 w3 w7 w5 g1a bx c1b sk0 sv0 g1e c1a c1e g2e c2b g3b c2e c2a g3e k10 c3e r10 c3b s10 k24 c3a r24 s22 s20 k30 s24 r30 s40 s42 s30 s14 s16 k44 k46 s34 s44 s36 s46 f3 f4",
+    "S": "lp1 lup lv e1 w2 w0 w6 g1b g2b g2a sv1 sk1 sv2 sk2 g3a sk3 sv3 k20 v20 k14 k40 v40 v14 k34 v34 f1 r44 f0 r46 f2 st2 st4",
+    "P": "m1b m1a m1e m2b m2e m2a m3e m3b m3a a10 x22 x20 a21 a20 a11 x40 x42 a23 a22 x14 a41 x16 a30 a31 a12 x34 x36 a40 a32 a42 a13 a33",
+    "Y": "lp0 lex lb lk lqa lqb st1 st0 st3",
+    "G": "im iz id ic sx sd0 sd1 sd2",
+}
+
+SCRATCH = {
+    "pc": ("sbuf", [128, 256], "int32"), "d1": ("sbuf", [128, 256], "int32"), "d2": ("sbuf", [128, 256], "int32"),
+    "d3": ("sbuf", [128, 256], "bfloat16"), "pw": ("sbuf", [128, 2432], "bfloat16"),
+    "upi": ("sbuf", [128, 128], "int32"), "exi": ("sbuf", [128, 8], "int32"), "exu": ("sbuf", [128, 8], "uint16"),
+    "el": ("sbuf", [128, 32], "uint16"), "ga4": ("sbuf", [128, 384], "bfloat16"),
+    "kw": ("sbuf", [128, 2560], "bfloat16"), "vw": ("sbuf", [128, 2560], "bfloat16"),
+    "qs": ("sbuf", [128, 2048], "bfloat16"), "bs": ("sbuf", [128, 4], "float32"), "bx": ("sbuf", [128, 4], "float32"),
+    "ys": ("sbuf", [128, 2048], "float32"), "sk": ("sbuf", [128, 512], "bfloat16"), "sv": ("sbuf", [128, 512], "bfloat16"),
+    "im": ("sbuf", [128, 8], "int32"), "iz": ("sbuf", [128, 8], "int32"), "im2": ("sbuf", [128, 8], "int32"),
+    "iz2": ("sbuf", [128, 8], "int32"), "ia": ("sbuf", [128, 4], "int32"), "cf": ("sbuf", [128, 4], "float32"),
+    "cb": ("sbuf", [128, 4], "float32"), "msk": ("sbuf", [128, 8], "float32"), "icol": ("sbuf", [128, 128], "float32"),
+    "idia": ("sbuf", [128, 128], "float32"), "zz": ("sbuf", [128, 144], "bfloat16"), "idh": ("sbuf", [128, 128], "float16"),
+    "idn": ("sbuf", [128, 128], "float16"), "idb": ("sbuf", [128, 128], "bfloat16"), "idx": ("sbuf", [128, 128], "bfloat16"),
+    "ea": ("psum", [128, 512], "float32"), "eb": ("psum", [128, 512], "float32"),
+    "xa": ("psum", [128, 512], "float32"), "xb": ("psum", [128, 512], "float32"),
+}
+for _d in range(1, 5):
+    SCRATCH["l%d" % _d] = ("sbuf", [128, 128], "uint16")
+    SCRATCH["xg%d" % _d] = ("sbuf", [128, 2048], "bfloat16")
+    SCRATCH["vg%d" % _d] = ("sbuf", [128, 2048], "bfloat16")
+    SCRATCH["pp%d" % _d] = ("sbuf", [128, 2048], "float16")
+    SCRATCH["acc%d" % (_d - 1)] = ("psum", [128, 512], "float32")
+    if _d < 4:
+        SCRATCH["ga%d" % _d] = ("sbuf", [128, 2048], "bfloat16")
+
+SEMAPHORES = (["cV", "cS", "cP", "cG", "lex", "lp0", "lp1", "lup", "lb", "lk", "lv", "lqa", "lqb", "sx", "ax"]
+              + ["sd%d" % i for i in range(4)] + ["ad%d" % i for i in range(4)] + ["st%d" % i for i in range(8)])
+
+
+def build(g, core, T, topo):
+    rank = T.rank_of(core)
+    serve, ask = rank < len(T.cores) - 1, rank > 0
+    ops = {}
+    V, S, P = g.vector, g.scalar, g.tensor
+    dq = {"S": g.scalar, "Y": g.sync}
+    styles = set(u[3] for u in UNITS)
+
+    def op(name, eng, kind, n, deps, fn, **kw):
+        ops[name] = dict(eng=eng, kind=kind, n=n, deps=list(deps), fn=fn, **kw)
+
+    def load(name, out, in_, nbytes, deps=()):
+        after = [QAFTER[name]] if name in QAFTER else []
+        op(name, "YS", "dma", nbytes, list(deps) + after, lambda e: dq[e].dma_start(out, in_), sem=name)
+
+    def scale(name, out, in_, n, s1, s2, deps, kind):
+        def fn(e):
+            if e == "V":
+                if s2 is None:
+                    if isinstance(s1, float) and s1 == 1.0:
+                        return V.tensor_copy(out, in_())
+                    return V.tensor_scalar(out, in_(), s1, None, ALU.mult)
+                return V.tensor_scalar(out, in_(), s1, s2, ALU.mult, ALU.add)
+            if s2 is None:
+                return S.activation(out, in_(), ACT.Identity, scale=s1)
+            return S.activation(out, in_(), ACT.Identity, bias=s2, scale=s1)
+        op(name, "VS", kind, n, deps, fn)
+
+    def ts(name, out, in0, s1, s2, o0, o1, n, deps):
+        if o1 is None:
+            op(name, "V", "f", n, deps, lambda e: V.tensor_scalar(out, in0, s1, None, o0))
+        else:
+            op(name, "V", "f", n, deps, lambda e: V.tensor_scalar(out, in0, s1, s2, o0, o1))
+
+    if ask:
+        load("lex", T.exi[:], T.ex[:], 4096)
+    load("lp0", T.pc[0:128:2, :], T.par[:], 65536)
+    load("lp1", T.pc[1:128:2, :], T.par[:], 65536)
+    load("lup", T.upi[:], T.up[:], 65536)
+    load("lb", T.bs[:], T.b[:], 2048)
+    load("lk", T.kw[:, 0:NT], T.k[:], 524288)
+    load("lv", T.vw[:, 0:NT], T.v[:], 524288)
+    load("lqa", T.qs[:, 0:1024], T.q[:, 0:1024], 262144)
+    load("lqb", T.qs[:, 1024:2048], T.q[:, 1024:2048], 262144)
+
+    op("iz", "G", "iota", 8, [], lambda e: g.iota(T.iz[:], [[-16, 8]], 0, 1))
+    op("im", "G", "iota", 8, [], lambda e: g.iota(T.im[:], [[-2, 8]], 16, 1))
+    op("ic", "G", "iota", 128, [], lambda e: g.iota(T.icol[:], [[1, 128]], 0, 0, allow_small_or_imprecise_dtypes=True))
+    op("id", "G", "iota", 128, [], lambda e: g.iota(T.idia[:], [[1, 128]], 0, -1, allow_small_or_imprecise_dtypes=True))
+    odd = T.ia[:, 0:1]
+    ts("ca", odd, T.iz[:, 0:1], 1, None, ALU.bitwise_and, None, 1, ["iz"])
+    ts("cm", T.cf[:, 0:1], odd, -127.0, 128.0, ALU.mult, ALU.add, 1, ["ca"])
+    ts("cw", T.cf[:, 1:2], odd, 127.0, 1.0, ALU.mult, ALU.add, 1, ["ca"])
+    ts("k1", T.im2[:], T.im[:], 14, None, ALU.bitwise_and, None, 8, ["im"])
+    ts("k2", T.msk[:], T.im2[:], 0.0, None, ALU.is_equal, None, 8, ["k1"])
+    op("z0", "V", "h", 144, [], lambda e: V.memset(T.zz[:], 0.0))
+    ts("z1", T.iz2[:], T.iz[:], 4, None, ALU.arith_shift_right, None, 8, ["iz"])
+    ts("z2", T.zz[:, 15:143:16], T.iz2[:], 0.0, T.cf[:, 1:2], ALU.is_equal, ALU.mult, 8, ["z0", "z1", "cw"])
+    ts("ih", T.idh[:], T.idia[:], 0.0, None, ALU.is_equal, None, 128, ["id"])
+    if "a" in styles:
+        ts("in", T.idn[:], T.idia[:], 0.0, -1.0, ALU.is_equal, ALU.mult, 128, ["id"])
+    if "d" in styles:
+        ts("ib", T.idb[:], T.idia[:], 0.0, None, ALU.is_equal, None, 128, ["id"])
+        ts("ix", T.idx[:], T.idia[:], 0.0, BIG, ALU.is_equal, ALU.mult, 128, ["id"])
+        ts("bx", T.bx[:], T.bs[:], BIG, None, ALU.mult, None, 4, ["lb"])
+    win = ["w%d" % i for i in range(8)]
+    if ask:
+        ts("cl", T.cf[:, 2:3], odd, -0.125, 0.125, ALU.mult, ALU.add, 1, ["ca"])
+        ts("cf", T.cf[:, 3:4], odd, 0.125, None, ALU.mult, None, 1, ["ca"])
+        ts("cb", T.cb[:, 0:3], T.icol[:, 17:20], T.cf[:, 3:4], None, ALU.mult, None, 3, ["cf", "ic"])
+        for t in range(3):
+            scale("e%d" % t, T.pw[:, NT + NE * t:NT + NE * (t + 1)], lambda: T.icol[:], 128, T.cf[:, 2:3], T.cb[:, t:t + 1],
+                  ["cl", "cb", "ic"], "f")
+            win.append("e%d" % t)
+    pend = NT + 3 * NE if ask else NT
+
+    ts("d1", T.d1[:], T.pc[:], T.cf[:, 0:1], None, ALU.mult, None, 256, ["lp0", "lp1", "cm"])
+    ts("d2", T.d2[:], T.d1[:], 7, 127, ALU.logical_shift_right, ALU.bitwise_and, 256, ["d1"])
+    op("d3", "V", "f", 256, ["d2"], lambda e: V.tensor_copy(T.d3[:], T.d2[:]))
+    for i in range(8):
+        scale("w%d" % i, T.pw[:, 256 * i:256 * (i + 1)], lambda: T.d3[:], 256, T.msk[:, i:i + 1], None, ["d3", "k2"], "h")
+    op("up", "V", "f", 128, ["lup"], lambda e: V.tensor_copy(T.l1[:], T.upi[:]))
+
+    def dst(r):
+        rid, pid, _ = topo.addr(T.cores[r])
+        return rid, pid, topo.engines(core, T.cores[r])[:NENG]
+
+    def bits(es):
+        return sum(1 << x for x in es)
+
+    xl = [T.el[:, 8 * t:8 * t + 8] for t in range(ND)]
+    xd = ["ax", "c1e", "c2e", "c3e"]
+    if ask:
+        op("xu", "V", "f", 8, ["lex"], lambda e: V.tensor_copy(T.exu[:], T.exi[:]))
+        rid, pid, es = dst(rank - 1)
+        op("sx", "G", "rem", 2048, ["xu"], lambda e: g.remote_dma(xl[0], T.exu[:], T.sem.ax, T.sem.sx, pid, rid, bits(es)),
+           tok=("sx", len(es)))
+    if serve:
+        op("ax", "", "arr", 0, ["sx"], None, tok=("ax", NENG))
+
+    def lift(name, lst, n, ga, base, bank, out, deps):
+        scale("g" + name, ga[:, base:base + 16 * n], lambda: T.pw[:, 0:pend].indirect(lst), 16 * n, 1.0, None, win + deps, "g")
+
+        def mm(e):
+            for i in range(16):
+                r = P.matmul(bank[:, 0:n], T.zz[:, 15 - i:143 - i], ga[:, base + i:base + 16 * n:16], i == 0, i == 15)
+            return r
+        op("m" + name, "P", "mm", 16 * max(64, n), ["g" + name, "z2"], mm)
+        op("c" + name, "V", "f", n, ["m" + name], lambda e: V.tensor_copy(out, bank[:, 0:n]))
+
+    have = {(1, 0): "up", (1, 1): "up"}
+    for lv in range(1, 4):
+        for h in range(2):
+            nm = "%d%s" % (lv, "ab"[h])
+            lift(nm, T["l%d" % lv][:, 64 * h:64 * h + 64], 64, T["ga%d" % lv], 1024 * h, (T.ea, T.eb)[h],
+                 T["l%d" % (lv + 1)][:, 64 * h:64 * h + 64], [have[(lv, h)]])
+            have[(lv + 1, h)] = "c" + nm
+
+    if serve:
+        for t in range(1, ND):
+            lift("%de" % t, xl[t - 1], 8, T.ga4, NE * (t - 1), T.acc3, xl[t], [xd[t - 1]])
+        for t in range(ND):
+            scale("sk%d" % t, T.sk[:, NE * t:NE * (t + 1)], lambda t=t: T.kw[:, 0:NT].indirect(xl[t]), NE, 1.0, None, ["lk", xd[t]], "g")
+            scale("sv%d" % t, T.sv[:, NE * t:NE * (t + 1)], lambda t=t: T.vw[:, 0:NT].indirect(xl[t]), NE, 1.0, None, ["lv", xd[t]], "g")
+        rid2, pid2, es2 = dst(rank + 1)
+        half = len(es2) // 2
+        for j, lv in enumerate(SENDS):
+            a, z = NE * lv[0], NE * (lv[-1] + 1)
+
+            def send(e, j=j, a=a, z=z):
+                return g.remote_dma_fused([
+                    RemoteDMATransfer(dst_ids=[DstId(rid=rid2, pnc=pid2)], dma_engine_mask=bits(m), remote_sem=T.sem["ad%d" % j],
+                                      src=s[:, a:z], dst=w[:, NT + a:NT + z])
+                    for s, w, m in ((T.sk, T.kw, es2[:half]), (T.sv, T.vw, es2[half:]))], local_sem=T.sem["sd%d" % j])
+            op("sd%d" % j, "G", "rem", 512 * (z - a), ["sk%d" % t for t in lv] + ["sv%d" % t for t in lv], send, tok=("sd%d" % j, len(es2)))
+    if ask:
+        for j in range(len(SENDS)):
+            op("ad%d" % j, "", "arr", 0, ["sd%d" % j], None, tok=("ad%d" % j, NENG))
+
+    fin = {}
+    for c0, c1, mode in FINALS:
+        for c in range(c0 // 256, c1 // 256):
+            fin[c] = mode
+    naccs = [3 + (fin[2 * c] == "S") for c in range(4)]
+    seen = [0, 0, 0, 0]
+    accs = [[], [], [], []]
+    made, minus, xq = {}, {}, []
+    for d, c0, c1, style in UNITS:
+        nm = "%d%d" % (d, c0 // 256)
+        n, h = c1 - c0, c0 // 1024
+        wend = NT + NE * d if ask else NT
+        lst = T["l%d" % d][:, c0 // 16:c1 // 16]
+        dep = [have[(d, h)]] + (["ad%d" % j for j, lv in enumerate(SENDS) if lv[0] < d] if ask else [])
+        xg, vg, pp = T["xg%d" % d], T["vg%d" % d], T["pp%d" % d]
+        if style == "a":
+            op("k" + nm, "V", "tg", n, dep + ["lk", "lq" + "ab"[h]], lambda e, x=xg[:, c0:c1], wend=wend, lst=lst, q=T.qs[:, c0:c1]:
+               V.tensor_tensor(x, T.kw[:, 0:wend].indirect(lst), q, ALU.subtract))
+
+            def relu(e, x=xg[:, c0:c1], b=T.bs[:, d - 1:d]):
+                if e == "V":
+                    return V.tensor_scalar(x, x, b, 0.0, ALU.subtract, ALU.min)
+                return S.activation(x, x, ACT.Relu, bias=b, scale=-1.0)
+            op("r" + nm, "VS", "h", n, ["k" + nm, "lb"], relu)
+            op("s" + nm, "V", "tg", n, dep + ["r" + nm, "lv"], lambda e, x=xg[:, c0:c1], p=pp[:, c0:c1], wend=wend, lst=lst:
+               V.tensor_tensor(p, T.vw[:, 0:wend].indirect(lst), x, ALU.mult))
+            for c in range(c0 // 256, c1 // 256):
+                made[(d, c)] = "s" + nm
+                minus[(d, c)] = "r" + nm in ORDER["V"].split()
+            continue
+        scale("v" + nm, vg[:, c0:c1], lambda wend=wend, lst=lst: T.vw[:, 0:wend].indirect(lst), n, TINY, None, dep + ["lv"], "g")
+        scale("k" + nm, xg[:, c0:c1], lambda wend=wend, lst=lst: T.kw[:, 0:wend].indirect(lst), n, -BIG, T.bx[:, d - 1:d],
+              dep + ["lk", "bx"], "g")
+        for a in range(c0, c1, 512):
+            z = min(a + 512, c1)
+            sn = "%d%d" % (d, a // 256)
+            bank = (T.xa, T.xb)[len(xq) % 2][:, 0:z - a]
+
+            def xm(e, bank=bank, xg=xg, a=a, z=z):
+                P.matmul(bank, T.idx[:], T.qs[:, a:z], True, False)
+                return P.matmul(bank, T.idb[:], xg[:, a:z], False, True)
+            op("x" + sn, "P", "mm", 2 * (z - a), ["k" + nm, "ib", "ix", "lq" + "ab"[h]] + xq[-2:-1], xm)
+            op("s" + sn, "V", "f", z - a, ["x" + sn, "v" + nm], lambda e, bank=bank, v=vg[:, a:z], p=pp[:, a:z]:
+               V.tensor_tensor_scan(p, bank, v, 0.0, ALU.max, ALU.mult))
+            xq.append("s" + sn)
+            for c in range(a // 256, z // 256):
+                made[(d, c)] = "s" + sn
+
+    for d in range(1, ND + 1):
+        for c in range(4):
+            if d <= naccs[c]:
+                def acc(e, d=d, c=c):
+                    seen[c] += 1
+                    return P.matmul(T["acc%d" % c][:], (T.idn if minus.get((d, 2 * c)) else T.idh)[:],
+                                    T["pp%d" % d][:, 512 * c:512 * c + 512], seen[c] == 1, seen[c] == naccs[c])
+                op("a%d%d" % (d, c), "P", "mm", 512,
+                   sorted(set([made[(d, 2 * c)], made[(d, 2 * c + 1)], "ih", "in"])) + (["c3e"] if c == 3 else []), acc)
+                accs[c].append("a%d%d" % (d, c))
+    for j, (c0, c1, mode) in enumerate(FINALS):
+        c = c0 // 512
+        bank = T["acc%d" % c][:, c0 - 512 * c:c1 - 512 * c]
+        if mode == "V":
+            op("f%d" % j, "V", "f", c1 - c0, accs[c] + sorted(set(made[(ND, x)] for x in range(c0 // 256, c1 // 256))),
+               lambda e, bank=bank, c0=c0, c1=c1: V.tensor_tensor(T.ys[:, c0:c1], bank, T.pp4[:, c0:c1],
+                                                                  ALU.subtract if minus.get((ND, c0 // 256)) else ALU.add))
+        else:
+            scale("f%d" % j, T.ys[:, c0:c1], lambda bank=bank: bank, c1 - c0, 1.0, None, accs[c], "f")
+        load("st%d" % j, T.y[:, c0:c1], T.ys[:, c0:c1], 512 * (c1 - c0), ["f%d" % j])
+    return ops
+
+
+def rank_program(g, core, T, topo):
+    if T.rank_of(core) is None:
+        return
+    ops = build(g, core, T, topo)
+    queue = {"V": g.vector, "S": g.scalar, "P": g.tensor, "Y": g.sync, "G": g}
+    order = {e: [n for n in ORDER[e].split() if n in ops] for e in queue}
+    tok, count, ends = {}, {}, []
+    for e in queue:
+        for n in order[e]:
+            o = ops[n]
+            if o["kind"] == "dma":
+                tok[n] = (o["sem"], 16)
+            elif o["kind"] == "rem":
+                tok[n] = o["tok"]
+                ends.append(tok[n])
+            else:
+                count[e] = count.get(e, 0) + 1
+                tok[n] = ("c" + e, count[e])
+    for n, o in ops.items():
+        if o["kind"] == "arr":
+            tok[n] = o["tok"]
+    assert all(n in tok for n in ops)
+    for e, q in queue.items():
+        waited = {}
+        for n in order[e]:
+            o = ops[n]
+            need = {}
+            for d in o["deps"]:
+                if d in tok:
+                    s, val = tok[d]
+                    need[s] = max(need.get(s, 0), val)
+            for s, val in need.items():
+                if waited.get(s, 0) < val:
+                    q.wait_ge(T.sem[s], val)
+                    waited[s] = val
+            ins = o["fn"](e)
+            if o["kind"] != "rem":
+                ins.then_inc(T.sem[tok[n][0]], 16 if o["kind"] == "dma" else 1)
+        if e == "Y":
+            for j in range(len(FINALS)):
+                q.wait_ge(T.sem["st%d" % j], 16)
+        if e == "G":
+            for s, val in ends + [("c" + x, count[x]) for x in count]:
+                if waited.get(s, 0) < val:
+                    q.wait_ge(T.sem[s], val)

@@ -7,24 +7,24 @@ NT, NE, ND = 2048, 128, 4
 BIG = float(2 ** 50)
 TINY = 1.0 / BIG
 
-UNITS = [(1, 0, 1024, "a"), (2, 0, 1024, "d"), (3, 0, 1024, "a"), (4, 0, 1024, "d"), (1, 1024, 2048, "d"),
-         (2, 1024, 2048, "a"), (3, 1024, 2048, "d"), (4, 1024, 1536, "a"), (4, 1536, 2048, "a")]
-FINALS = [(0, 512, "S"), (512, 1024, "S"), (1024, 1536, "S"), (1536, 1792, "V"), (1792, 2048, "V")]
+UNITS = [(1, 0, 1024, "a"), (1, 1024, 2048, "d"), (2, 0, 1024, "d"), (3, 0, 1024, "a"), (4, 0, 1024, "d"), (2, 1024, 2048, "a"),
+         (3, 1024, 1536, "d"), (4, 1024, 1536, "a"), (3, 1536, 2048, "d"), (4, 1536, 2048, "a")]
+FINALS = [(0, 512, "S"), (512, 1024, "S"), (1024, 1536, "S"), (1536, 2048, "V")]
 SENDS = [[0], [1], [2, 3]]
 NENG = 8
 QAFTER = {"lqa": "sx", "lqb": "sd0"}
 ORDER = {
-    "V": "z0 k1 ca cl cf cw z1 k2 cm cb z2 e0 e2 ix ih in ib d1 xu d2 up d3 w1 w4 w3 w7 w5 g1a bx c1b sk0 sv0 g1e c1a c1e g2e c2b g3b c2e c2a g3e k10 c3e r10 c3b s10 k24 c3a r24 s22 s20 k30 s24 r30 s40 s42 s30 s14 s16 k44 k46 s34 s44 s36 s46 f3 f4",
-    "S": "lp1 lup lv e1 w2 w0 w6 g1b g2b g2a sv1 sk1 sv2 sk2 g3a sk3 sv3 k20 v20 k14 k40 v40 v14 k34 v34 f1 r44 f0 r46 f2 st2 st4",
-    "P": "m1b m1a m1e m2b m2e m2a m3e m3b m3a a10 x22 x20 a21 a20 a11 x40 x42 a23 a22 x14 a41 x16 a30 a31 a12 x34 x36 a40 a32 a42 a13 a33",
+    "V": "z0 k1 ca cm k2 cl cf cw z1 cb z2 e0 ix ih in ib d1 d2 d3 up w1 w4 w3 w7 w5 g1a xu sv0 g1e c1b c1a bx c1e g2a c2b c2e sv2 g3e c2a k10 c3e r10 c3b s10 k24 s16 r24 s14 s24 c3a k30 s22 r30 s20 s30 s42 s40 k44 k46 s34 s44 s36 s46 f3",
+    "S": "lp1 lup lv e1 e2 w2 w0 w6 g1b sk0 g2b sv1 g2e sk1 g3b sk2 k14 sk3 sv3 v14 g3a k20 v20 k40 v40 k36 v34 k34 f1 r44 f0 v36 r46 f2 st2",
+    "P": "m1b m1a m1e m2b m2e m2a m3e m3b x16 x14 m3a a13 a10 a11 x22 x20 x42 a23 a21 x40 a20 a12 a30 a31 a41 a40 x34 x36 a22 a32 a42 a33",
     "Y": "lp0 lex lb lk lqa lqb st1 st0 st3",
-    "G": "im iz id ic sx sd0 sd1 sd2",
+    "G": "im iz ic id sx sd0 sd1 sd2",
 }
 
 SCRATCH = {
     "pc": ("sbuf", [128, 256], "int32"), "d1": ("sbuf", [128, 256], "int32"), "d2": ("sbuf", [128, 256], "int32"),
     "d3": ("sbuf", [128, 256], "bfloat16"), "pw": ("sbuf", [128, 2432], "bfloat16"),
-    "upi": ("sbuf", [128, 128], "int32"), "exi": ("sbuf", [128, 8], "int32"), "exu": ("sbuf", [128, 8], "uint16"),
+    "upi": ("sbuf", [128, 128], "int32"), "exi": ("sbuf", [128, 8], "int32"), "exr": ("sbuf", [128, 8], "int32"),
     "el": ("sbuf", [128, 32], "uint16"), "ga4": ("sbuf", [128, 384], "bfloat16"),
     "kw": ("sbuf", [128, 2560], "bfloat16"), "vw": ("sbuf", [128, 2560], "bfloat16"),
     "qs": ("sbuf", [128, 2048], "bfloat16"), "bs": ("sbuf", [128, 4], "float32"), "bx": ("sbuf", [128, 4], "float32"),
@@ -141,14 +141,14 @@ def build(g, core, T, topo):
         return sum(1 << x for x in es)
 
     xl = [T.el[:, 8 * t:8 * t + 8] for t in range(ND)]
-    xd = ["ax", "c1e", "c2e", "c3e"]
+    xd = ["xu", "c1e", "c2e", "c3e"]
     if ask:
-        op("xu", "V", "f", 8, ["lex"], lambda e: V.tensor_copy(T.exu[:], T.exi[:]))
         rid, pid, es = dst(rank - 1)
-        op("sx", "G", "rem", 2048, ["xu"], lambda e: g.remote_dma(xl[0], T.exu[:], T.sem.ax, T.sem.sx, pid, rid, bits(es)),
+        op("sx", "G", "rem", 2048, ["lex"], lambda e: g.remote_dma(T.exr[:], T.exi[:], T.sem.ax, T.sem.sx, pid, rid, bits(es)),
            tok=("sx", len(es)))
     if serve:
         op("ax", "", "arr", 0, ["sx"], None, tok=("ax", NENG))
+        op("xu", "V", "f", 8, ["ax"], lambda e: V.tensor_copy(xl[0], T.exr[:]))
 
     def lift(name, lst, n, ga, base, bank, out, deps):
         scale("g" + name, ga[:, base:base + 16 * n], lambda: T.pw[:, 0:pend].indirect(lst), 16 * n, 1.0, None, win + deps, "g")
@@ -191,7 +191,7 @@ def build(g, core, T, topo):
 
     fin = {}
     for c0, c1, mode in FINALS:
-        for c in range(c0 // 256, c1 // 256):
+        for c in range(c0 // 256, (c1 + 255) // 256):
             fin[c] = mode
     naccs = [3 + (fin[2 * c] == "S") for c in range(4)]
     seen = [0, 0, 0, 0]
@@ -251,7 +251,7 @@ def build(g, core, T, topo):
         c = c0 // 512
         bank = T["acc%d" % c][:, c0 - 512 * c:c1 - 512 * c]
         if mode == "V":
-            op("f%d" % j, "V", "f", c1 - c0, accs[c] + sorted(set(made[(ND, x)] for x in range(c0 // 256, c1 // 256))),
+            op("f%d" % j, "V", "f", c1 - c0, accs[c] + sorted(set(made[(ND, x)] for x in range(c0 // 256, (c1 + 255) // 256))),
                lambda e, bank=bank, c0=c0, c1=c1: V.tensor_tensor(T.ys[:, c0:c1], bank, T.pp4[:, c0:c1],
                                                                   ALU.subtract if minus.get((ND, c0 // 256)) else ALU.add))
         else:

@@ -7,18 +7,30 @@ NT, NE, ND = 2048, 128, 4
 BIG = float(2 ** 50)
 TINY = 1.0 / BIG
 
-UNITS = [(1, 0, 1024, "a"), (1, 1024, 2048, "d"), (2, 0, 1024, "d"), (3, 0, 1024, "a"), (4, 0, 1024, "d"), (2, 1024, 2048, "a"),
-         (3, 1024, 1536, "d"), (4, 1024, 1536, "a"), (3, 1536, 2048, "d"), (4, 1536, 2048, "a")]
+LIFTS = {1: [0, 1024, 2048], 2: [0, 1024, 2048], 3: [0, 1024, 2048]}
+UNITS = [(1, 0, 1024, "a"), (1, 1024, 2048, "e"), (2, 0, 1024, "e"), (3, 0, 1024, "a"), (4, 0, 1024, "e"), (2, 1024, 2048, "a"),
+         (3, 1024, 1536, "e"), (4, 1024, 1536, "a"), (3, 1536, 2048, "e"), (4, 1536, 2048, "a")]
 FINALS = [(0, 512, "S"), (512, 1024, "S"), (1024, 1536, "S"), (1536, 2048, "V")]
 SENDS = [[0], [1], [2, 3]]
 NENG = 8
-QAFTER = {"lqa": "sx", "lqb": "sd0"}
+AFTER = {"lqa": ["sx"], "lqb": ["sd0"]}
 ORDER = {
-    "V": "z0 k1 ca cm k2 cl cf cw z1 cb z2 e0 ix ih in ib d1 d2 d3 up w1 w4 w3 w7 w5 g1a xu sv0 g1e c1b c1a bx c1e g2a c2b c2e sv2 g3e c2a k10 c3e r10 c3b s10 k24 s16 r24 s14 s24 c3a k30 s22 r30 s20 s30 s42 s40 k44 k46 s34 s44 s36 s46 f3",
-    "S": "lp1 lup lv e1 e2 w2 w0 w6 g1b sk0 g2b sv1 g2e sk1 g3b sk2 k14 sk3 sv3 v14 g3a k20 v20 k40 v40 k36 v34 k34 f1 r44 f0 v36 r46 f2 st2",
-    "P": "m1b m1a m1e m2b m2e m2a m3e m3b x16 x14 m3a a13 a10 a11 x22 x20 x42 a23 a21 x40 a20 a12 a30 a31 a41 a40 x34 x36 a22 a32 a42 a33",
-    "Y": "lp0 lex lb lk lqa lqb st1 st0 st3",
-    "G": "im iz ic id sx sd0 sd1 sd2",
+    "V": "z0 ca cl k1 k2 cf z1 cm k3 cb cw d1 d2 d3 w2 w7 up w6 w0 w3 z2 g1a in xu sv0 c1b g1e c1a g2a c1e qa0 c2a c2e g3e sk1 c2b c3e k10 qa1 r10 k24 c3b r24 c3a k30 k44 s10 s24 r44 r30 s20 s30 k46 s40 s14 s44 s34 r46 s36 s46 f3",
+    "S": "lp1 lup lv e1 e2 e0 w1 w5 w4 g1b sk0 g2b bb g2e sv1 bx g3a sk2 sv2 g3b k14 k20 k40 v20 k36 k34 v40 v14 v34 v36 f1 f0 f2",
+    "P": "m1b m1a m1e m2a m2e m2b m3e m3a m3b a30 a21 a20 a31 a11 a41 a40 a10 a12 a42 a22 a32 a23 a13 a33",
+    "Y": "lp0 lex lb lk lqa lqb st1 st0 st2 st3",
+    "G": "iz im id ic sx sd0 sd1 sd2 r14 r20 r40 r34 r36",
+}
+
+UNITS = [(1, 0, 1024, "a"), (1, 1024, 2048, "e"), (2, 0, 1024, "e"), (3, 0, 1024, "a"), (4, 0, 1024, "e"), (2, 1024, 2048, "a"),
+         (3, 1024, 2048, "e"), (4, 1024, 1536, "a"), (4, 1536, 1792, "a"), (4, 1792, 2048, "a")]
+FINALS = [(0, 512, "S"), (512, 1024, "S"), (1024, 1536, "S"), (1536, 1792, "V"), (1792, 2048, "V")]
+ORDER = {
+    "V": "z0 ca cl cf cb cm k1 k2 z1 k3 d1 d2 d3 w2 up w5 w1 w7 w6 in cw z2 g1a xu sv0 c1b c1a g2a c1e c2b c2e g3e qa0 c2a sv1 c3e k10 c3b r10 qa1 c3a s10 k24 k30 r24 k44 r30 s24 s30 s20 s40 k46 s14 r44 s44 s34 k47 r47 s47 f4 r46 s46 f3",
+    "S": "lp1 lup lv e1 e2 e0 w3 w4 w0 bb g1b sk0 g1e bx g2b g2e sk1 g3b g3a sk2 sv2 k14 k20 k40 k34 v40 v20 v14 v34 f0 f1 f2 st2",
+    "P": "m1b m1a m1e m2b m2e m2a m3e m3b m3a a10 a22 a30 a21 a11 a23 a31 a20 a40 a13 a41 a42 a12 a32 a33",
+    "Y": "lp0 lex lb lk lqa lqb st0 st1 st4 st3",
+    "G": "iz ic im id sx sd0 sd1 sd2 r14 r20 r40 r34",
 }
 
 SCRATCH = {
@@ -27,15 +39,15 @@ SCRATCH = {
     "upi": ("sbuf", [128, 128], "int32"), "exi": ("sbuf", [128, 8], "int32"), "exr": ("sbuf", [128, 8], "int32"),
     "el": ("sbuf", [128, 32], "uint16"), "ga4": ("sbuf", [128, 384], "bfloat16"),
     "kw": ("sbuf", [128, 2560], "bfloat16"), "vw": ("sbuf", [128, 2560], "bfloat16"),
-    "qs": ("sbuf", [128, 2048], "bfloat16"), "bs": ("sbuf", [128, 4], "float32"), "bx": ("sbuf", [128, 4], "float32"),
+    "qs": ("sbuf", [128, 2048], "bfloat16"), "qa": ("sbuf", [128, 2048], "bfloat16"),
+    "bs": ("sbuf", [128, 4], "float32"), "bx": ("sbuf", [128, 4], "float32"), "bb": ("sbuf", [128, 4], "bfloat16"),
     "ys": ("sbuf", [128, 2048], "float32"), "sk": ("sbuf", [128, 512], "bfloat16"), "sv": ("sbuf", [128, 512], "bfloat16"),
     "im": ("sbuf", [128, 8], "int32"), "iz": ("sbuf", [128, 8], "int32"), "im2": ("sbuf", [128, 8], "int32"),
     "iz2": ("sbuf", [128, 8], "int32"), "ia": ("sbuf", [128, 4], "int32"), "cf": ("sbuf", [128, 4], "float32"),
-    "cb": ("sbuf", [128, 4], "float32"), "msk": ("sbuf", [128, 8], "float32"), "icol": ("sbuf", [128, 128], "float32"),
-    "idia": ("sbuf", [128, 128], "float32"), "zz": ("sbuf", [128, 144], "bfloat16"), "idh": ("sbuf", [128, 128], "float16"),
-    "idn": ("sbuf", [128, 128], "float16"), "idb": ("sbuf", [128, 128], "bfloat16"), "idx": ("sbuf", [128, 128], "bfloat16"),
-    "ea": ("psum", [128, 512], "float32"), "eb": ("psum", [128, 512], "float32"),
-    "xa": ("psum", [128, 512], "float32"), "xb": ("psum", [128, 512], "float32"),
+    "cb": ("sbuf", [128, 4], "float32"), "msk": ("sbuf", [128, 8], "float32"), "mskb": ("sbuf", [128, 8], "bfloat16"),
+    "icol": ("sbuf", [128, 128], "float32"), "idia": ("sbuf", [128, 128], "float32"),
+    "zz": ("sbuf", [128, 144], "bfloat16"), "idn": ("sbuf", [128, 128], "float16"),
+    "idb": ("sbuf", [128, 128], "bfloat16"), "idx": ("sbuf", [128, 128], "bfloat16"),
 }
 for _d in range(1, 5):
     SCRATCH["l%d" % _d] = ("sbuf", [128, 128], "uint16")
@@ -43,11 +55,12 @@ for _d in range(1, 5):
     SCRATCH["vg%d" % _d] = ("sbuf", [128, 2048], "bfloat16")
     SCRATCH["pp%d" % _d] = ("sbuf", [128, 2048], "float16")
     SCRATCH["acc%d" % (_d - 1)] = ("psum", [128, 512], "float32")
+    SCRATCH["up%d" % (_d - 1)] = ("psum", [128, 512], "float32")
     if _d < 4:
         SCRATCH["ga%d" % _d] = ("sbuf", [128, 2048], "bfloat16")
 
 SEMAPHORES = (["cV", "cS", "cP", "cG", "lex", "lp0", "lp1", "lup", "lb", "lk", "lv", "lqa", "lqb", "sx", "ax"]
-              + ["sd%d" % i for i in range(4)] + ["ad%d" % i for i in range(4)] + ["st%d" % i for i in range(8)])
+              + ["%s%d" % (n, i) for n in ("sd", "ad", "st") for i in range(8)] + ["dx%d" % i for i in range(16)])
 
 
 def build(g, core, T, topo):
@@ -56,18 +69,18 @@ def build(g, core, T, topo):
     ops = {}
     V, S, P = g.vector, g.scalar, g.tensor
     dq = {"S": g.scalar, "Y": g.sync}
-    styles = set(u[3] for u in UNITS)
 
-    def op(name, eng, kind, n, deps, fn, **kw):
-        ops[name] = dict(eng=eng, kind=kind, n=n, deps=list(deps), fn=fn, **kw)
+    def op(name, eng, kind, deps, fn, **kw):
+        ops[name] = dict(eng=eng, kind=kind, deps=list(deps), fn=fn, **kw)
 
-    def load(name, out, in_, nbytes, deps=()):
-        after = [QAFTER[name]] if name in QAFTER else []
-        op(name, "YS", "dma", nbytes, list(deps) + after, lambda e: dq[e].dma_start(out, in_), sem=name)
+    def load(name, out, in_, deps=()):
+        op(name, "YS", "dma", list(deps) + AFTER.get(name, []), lambda e: dq[e].dma_start(out, in_), sem=name)
 
-    def scale(name, out, in_, n, s1, s2, deps, kind):
+    def scale(name, out, in_, s1, s2, deps, narrow=None):
         def fn(e):
             if e == "V":
+                if narrow is not None:
+                    return V.tensor_scalar(out, in_(), narrow, None, ALU.mult)
                 if s2 is None:
                     if isinstance(s1, float) and s1 == 1.0:
                         return V.tensor_copy(out, in_())
@@ -76,62 +89,65 @@ def build(g, core, T, topo):
             if s2 is None:
                 return S.activation(out, in_(), ACT.Identity, scale=s1)
             return S.activation(out, in_(), ACT.Identity, bias=s2, scale=s1)
-        op(name, "VS", kind, n, deps, fn)
+        op(name, "VS", "c", deps, fn)
 
-    def ts(name, out, in0, s1, s2, o0, o1, n, deps):
+    def ts(name, out, in0, s1, s2, o0, o1, deps):
         if o1 is None:
-            op(name, "V", "f", n, deps, lambda e: V.tensor_scalar(out, in0, s1, None, o0))
+            op(name, "V", "c", deps, lambda e: V.tensor_scalar(out, in0, s1, None, o0))
         else:
-            op(name, "V", "f", n, deps, lambda e: V.tensor_scalar(out, in0, s1, s2, o0, o1))
+            op(name, "V", "c", deps, lambda e: V.tensor_scalar(out, in0, s1, s2, o0, o1))
 
     if ask:
-        load("lex", T.exi[:], T.ex[:], 4096)
-    load("lp0", T.pc[0:128:2, :], T.par[:], 65536)
-    load("lp1", T.pc[1:128:2, :], T.par[:], 65536)
-    load("lup", T.upi[:], T.up[:], 65536)
-    load("lb", T.bs[:], T.b[:], 2048)
-    load("lk", T.kw[:, 0:NT], T.k[:], 524288)
-    load("lv", T.vw[:, 0:NT], T.v[:], 524288)
-    load("lqa", T.qs[:, 0:1024], T.q[:, 0:1024], 262144)
-    load("lqb", T.qs[:, 1024:2048], T.q[:, 1024:2048], 262144)
+        load("lex", T.exi[:], T.ex[:])
+    load("lp0", T.pc[0:128:2, :], T.par[:])
+    load("lp1", T.pc[1:128:2, :], T.par[:])
+    load("lup", T.upi[:], T.up[:])
+    load("lb", T.bs[:], T.b[:])
+    load("lk", T.kw[:, 0:NT], T.k[:])
+    load("lv", T.vw[:, 0:NT], T.v[:])
+    load("lqa", T.qs[:, 0:1024], T.q[:, 0:1024])
+    load("lqb", T.qs[:, 1024:2048], T.q[:, 1024:2048])
 
-    op("iz", "G", "iota", 8, [], lambda e: g.iota(T.iz[:], [[-16, 8]], 0, 1))
-    op("im", "G", "iota", 8, [], lambda e: g.iota(T.im[:], [[-2, 8]], 16, 1))
-    op("ic", "G", "iota", 128, [], lambda e: g.iota(T.icol[:], [[1, 128]], 0, 0, allow_small_or_imprecise_dtypes=True))
-    op("id", "G", "iota", 128, [], lambda e: g.iota(T.idia[:], [[1, 128]], 0, -1, allow_small_or_imprecise_dtypes=True))
+    op("iz", "G", "c", [], lambda e: g.iota(T.iz[:], [[-16, 8]], 0, 1))
+    op("im", "G", "c", [], lambda e: g.iota(T.im[:], [[-2, 8]], 16, 1))
+    op("ic", "G", "c", [], lambda e: g.iota(T.icol[:], [[1, 128]], 0, 0, allow_small_or_imprecise_dtypes=True))
+    op("id", "G", "c", [], lambda e: g.iota(T.idia[:], [[1, 128]], 0, -1, allow_small_or_imprecise_dtypes=True))
     odd = T.ia[:, 0:1]
-    ts("ca", odd, T.iz[:, 0:1], 1, None, ALU.bitwise_and, None, 1, ["iz"])
-    ts("cm", T.cf[:, 0:1], odd, -127.0, 128.0, ALU.mult, ALU.add, 1, ["ca"])
-    ts("cw", T.cf[:, 1:2], odd, 127.0, 1.0, ALU.mult, ALU.add, 1, ["ca"])
-    ts("k1", T.im2[:], T.im[:], 14, None, ALU.bitwise_and, None, 8, ["im"])
-    ts("k2", T.msk[:], T.im2[:], 0.0, None, ALU.is_equal, None, 8, ["k1"])
-    op("z0", "V", "h", 144, [], lambda e: V.memset(T.zz[:], 0.0))
-    ts("z1", T.iz2[:], T.iz[:], 4, None, ALU.arith_shift_right, None, 8, ["iz"])
-    ts("z2", T.zz[:, 15:143:16], T.iz2[:], 0.0, T.cf[:, 1:2], ALU.is_equal, ALU.mult, 8, ["z0", "z1", "cw"])
-    ts("ih", T.idh[:], T.idia[:], 0.0, None, ALU.is_equal, None, 128, ["id"])
-    if "a" in styles:
-        ts("in", T.idn[:], T.idia[:], 0.0, -1.0, ALU.is_equal, ALU.mult, 128, ["id"])
-    if "d" in styles:
-        ts("ib", T.idb[:], T.idia[:], 0.0, None, ALU.is_equal, None, 128, ["id"])
-        ts("ix", T.idx[:], T.idia[:], 0.0, BIG, ALU.is_equal, ALU.mult, 128, ["id"])
-        ts("bx", T.bx[:], T.bs[:], BIG, None, ALU.mult, None, 4, ["lb"])
+    ts("ca", odd, T.iz[:, 0:1], 1, None, ALU.bitwise_and, None, ["iz"])
+    ts("cm", T.cf[:, 0:1], odd, -127.0, 128.0, ALU.mult, ALU.add, ["ca"])
+    ts("cw", T.cf[:, 1:2], odd, 127.0, 1.0, ALU.mult, ALU.add, ["ca"])
+    ts("k1", T.im2[:], T.im[:], 14, None, ALU.bitwise_and, None, ["im"])
+    ts("k2", T.msk[:], T.im2[:], 0.0, None, ALU.is_equal, None, ["k1"])
+    ts("k3", T.mskb[:], T.im2[:], 0.0, None, ALU.is_equal, None, ["k1"])
+    op("z0", "V", "c", [], lambda e: V.memset(T.zz[:], 0.0))
+    ts("z1", T.iz2[:], T.iz[:], 4, None, ALU.arith_shift_right, None, ["iz"])
+    ts("z2", T.zz[:, 15:143:16], T.iz2[:], 0.0, T.cf[:, 1:2], ALU.is_equal, ALU.mult, ["z0", "z1", "cw"])
+    ts("in", T.idn[:], T.idia[:], 0.0, -1.0, ALU.is_equal, ALU.mult, ["id"])
+    if any(u[3] == "d" for u in UNITS):
+        ts("ib", T.idb[:], T.idia[:], 0.0, None, ALU.is_equal, None, ["id"])
+        scale("ix", T.idx[:], lambda: T.idb[:], BIG, None, ["ib"])
+    scale("bb", T.bb[:], lambda: T.bs[:], 1.0, None, ["lb"])
+    scale("bx", T.bx[:], lambda: T.bs[:], BIG, None, ["lb"])
+    for h in range(2):
+        used = [c for u in UNITS if u[3] == "e" and u[1] // 1024 == h for c in u[1:3]]
+        if used:
+            scale("qa%d" % h, T.qa[:, min(used):max(used)], lambda a=min(used), z=max(used): T.qs[:, a:z], BIG, None, ["lq" + "ab"[h]])
     win = ["w%d" % i for i in range(8)]
     if ask:
-        ts("cl", T.cf[:, 2:3], odd, -0.125, 0.125, ALU.mult, ALU.add, 1, ["ca"])
-        ts("cf", T.cf[:, 3:4], odd, 0.125, None, ALU.mult, None, 1, ["ca"])
-        ts("cb", T.cb[:, 0:3], T.icol[:, 17:20], T.cf[:, 3:4], None, ALU.mult, None, 3, ["cf", "ic"])
+        ts("cl", T.cf[:, 2:3], odd, -0.125, 0.125, ALU.mult, ALU.add, ["ca"])
+        ts("cf", T.cf[:, 3:4], odd, 0.125, None, ALU.mult, None, ["ca"])
+        ts("cb", T.cb[:, 0:3], T.icol[:, 17:20], T.cf[:, 3:4], None, ALU.mult, None, ["cf", "ic"])
         for t in range(3):
-            scale("e%d" % t, T.pw[:, NT + NE * t:NT + NE * (t + 1)], lambda: T.icol[:], 128, T.cf[:, 2:3], T.cb[:, t:t + 1],
-                  ["cl", "cb", "ic"], "f")
+            scale("e%d" % t, T.pw[:, NT + NE * t:NT + NE * (t + 1)], lambda: T.icol[:], T.cf[:, 2:3], T.cb[:, t:t + 1], ["cl", "cb", "ic"])
             win.append("e%d" % t)
     pend = NT + 3 * NE if ask else NT
 
-    ts("d1", T.d1[:], T.pc[:], T.cf[:, 0:1], None, ALU.mult, None, 256, ["lp0", "lp1", "cm"])
-    ts("d2", T.d2[:], T.d1[:], 7, 127, ALU.logical_shift_right, ALU.bitwise_and, 256, ["d1"])
-    op("d3", "V", "f", 256, ["d2"], lambda e: V.tensor_copy(T.d3[:], T.d2[:]))
+    ts("d1", T.d1[:], T.pc[:], T.cf[:, 0:1], None, ALU.mult, None, ["lp0", "lp1", "cm"])
+    ts("d2", T.d2[:], T.d1[:], 7, 127, ALU.logical_shift_right, ALU.bitwise_and, ["d1"])
+    op("d3", "V", "c", ["d2"], lambda e: V.tensor_copy(T.d3[:], T.d2[:]))
     for i in range(8):
-        scale("w%d" % i, T.pw[:, 256 * i:256 * (i + 1)], lambda: T.d3[:], 256, T.msk[:, i:i + 1], None, ["d3", "k2"], "h")
-    op("up", "V", "f", 128, ["lup"], lambda e: V.tensor_copy(T.l1[:], T.upi[:]))
+        scale("w%d" % i, T.pw[:, 256 * i:256 * (i + 1)], lambda: T.d3[:], T.msk[:, i:i + 1], None, ["d3", "k2", "k3"], T.mskb[:, i:i + 1])
+    op("up", "V", "c", ["lup"], lambda e: V.tensor_copy(T.l1[:], T.upi[:]))
 
     def dst(r):
         rid, pid, _ = topo.addr(T.cores[r])
@@ -140,123 +156,114 @@ def build(g, core, T, topo):
     def bits(es):
         return sum(1 << x for x in es)
 
-    xl = [T.el[:, 8 * t:8 * t + 8] for t in range(ND)]
     xd = ["xu", "c1e", "c2e", "c3e"]
     if ask:
         rid, pid, es = dst(rank - 1)
-        op("sx", "G", "rem", 2048, ["lex"], lambda e: g.remote_dma(T.exr[:], T.exi[:], T.sem.ax, T.sem.sx, pid, rid, bits(es)),
+        op("sx", "G", "rem", ["lex"], lambda e: g.remote_dma(T.exr[:], T.exi[:], T.sem.ax, T.sem.sx, pid, rid, bits(es)),
            tok=("sx", len(es)))
     if serve:
-        op("ax", "", "arr", 0, ["sx"], None, tok=("ax", NENG))
-        op("xu", "V", "f", 8, ["ax"], lambda e: V.tensor_copy(xl[0], T.exr[:]))
+        op("ax", "", "arr", ["sx"], None, tok=("ax", NENG))
+        op("xu", "V", "c", ["ax"], lambda e: V.tensor_copy(T.el[:, 0:8], T.exr[:]))
 
     def lift(name, lst, n, ga, base, bank, out, deps):
-        scale("g" + name, ga[:, base:base + 16 * n], lambda: T.pw[:, 0:pend].indirect(lst), 16 * n, 1.0, None, win + deps, "g")
+        scale("g" + name, ga[:, base:base + 16 * n], lambda: T.pw[:, 0:pend].indirect(lst), 1.0, None, win + deps)
 
         def mm(e):
             for i in range(16):
                 r = P.matmul(bank[:, 0:n], T.zz[:, 15 - i:143 - i], ga[:, base + i:base + 16 * n:16], i == 0, i == 15)
             return r
-        op("m" + name, "P", "mm", 16 * max(64, n), ["g" + name, "z2"], mm)
-        op("c" + name, "V", "f", n, ["m" + name], lambda e: V.tensor_copy(out, bank[:, 0:n]))
+        op("m" + name, "P", "c", ["g" + name, "z2", "c%d%s" % (int(name[0]) - 1, name[1])], mm)
+        op("c" + name, "V", "c", ["m" + name], lambda e: V.tensor_copy(out, bank[:, 0:n]))
 
-    have = {(1, 0): "up", (1, 1): "up"}
-    for lv in range(1, 4):
-        for h in range(2):
-            nm = "%d%s" % (lv, "ab"[h])
-            lift(nm, T["l%d" % lv][:, 64 * h:64 * h + 64], 64, T["ga%d" % lv], 1024 * h, (T.ea, T.eb)[h],
-                 T["l%d" % (lv + 1)][:, 64 * h:64 * h + 64], [have[(lv, h)]])
-            have[(lv + 1, h)] = "c" + nm
+    def have(d, a, z):
+        if d == 1:
+            return ["up"]
+        cuts = LIFTS[d - 1]
+        return ["c%d%s" % (d - 1, "abcd"[i]) for i in range(len(cuts) - 1) if cuts[i] < z and a < cuts[i + 1]]
+
+    for lv, cuts in LIFTS.items():
+        for i, (a, z) in enumerate(zip(cuts, cuts[1:])):
+            lift("%d%s" % (lv, "abcd"[i]), T["l%d" % lv][:, a // 16:z // 16], (z - a) // 16, T["ga%d" % lv], a, T["up%d" % i],
+                 T["l%d" % (lv + 1)][:, a // 16:z // 16], have(lv, a, z))
 
     if serve:
         for t in range(1, ND):
-            lift("%de" % t, xl[t - 1], 8, T.ga4, NE * (t - 1), T.acc3, xl[t], [xd[t - 1]])
-        for t in range(ND):
-            scale("sk%d" % t, T.sk[:, NE * t:NE * (t + 1)], lambda t=t: T.kw[:, 0:NT].indirect(xl[t]), NE, 1.0, None, ["lk", xd[t]], "g")
-            scale("sv%d" % t, T.sv[:, NE * t:NE * (t + 1)], lambda t=t: T.vw[:, 0:NT].indirect(xl[t]), NE, 1.0, None, ["lv", xd[t]], "g")
+            lift("%de" % t, T.el[:, 8 * t - 8:8 * t], 8, T.ga4, NE * (t - 1), T.acc3, T.el[:, 8 * t:8 * t + 8], [xd[t - 1]])
         rid2, pid2, es2 = dst(rank + 1)
         half = len(es2) // 2
         for j, lv in enumerate(SENDS):
             a, z = NE * lv[0], NE * (lv[-1] + 1)
+            lst = T.el[:, a // 16:z // 16]
+            scale("sk%d" % j, T.sk[:, a:z], lambda lst=lst: T.kw[:, 0:NT].indirect(lst), 1.0, None, ["lk"] + [xd[t] for t in lv])
+            scale("sv%d" % j, T.sv[:, a:z], lambda lst=lst: T.vw[:, 0:NT].indirect(lst), 1.0, None, ["lv"] + [xd[t] for t in lv])
 
             def send(e, j=j, a=a, z=z):
                 return g.remote_dma_fused([
                     RemoteDMATransfer(dst_ids=[DstId(rid=rid2, pnc=pid2)], dma_engine_mask=bits(m), remote_sem=T.sem["ad%d" % j],
                                       src=s[:, a:z], dst=w[:, NT + a:NT + z])
                     for s, w, m in ((T.sk, T.kw, es2[:half]), (T.sv, T.vw, es2[half:]))], local_sem=T.sem["sd%d" % j])
-            op("sd%d" % j, "G", "rem", 512 * (z - a), ["sk%d" % t for t in lv] + ["sv%d" % t for t in lv], send, tok=("sd%d" % j, len(es2)))
+            op("sd%d" % j, "G", "rem", ["sk%d" % j, "sv%d" % j], send, tok=("sd%d" % j, len(es2)))
     if ask:
         for j in range(len(SENDS)):
-            op("ad%d" % j, "", "arr", 0, ["sd%d" % j], None, tok=("ad%d" % j, NENG))
+            op("ad%d" % j, "", "arr", ["sd%d" % j], None, tok=("ad%d" % j, NENG))
 
-    fin = {}
-    for c0, c1, mode in FINALS:
-        for c in range(c0 // 256, (c1 + 255) // 256):
-            fin[c] = mode
-    naccs = [3 + (fin[2 * c] == "S") for c in range(4)]
-    seen = [0, 0, 0, 0]
-    accs = [[], [], [], []]
-    made, minus, xq = {}, {}, []
+    made, nadd, xq = {}, 0, []
     for d, c0, c1, style in UNITS:
         nm = "%d%d" % (d, c0 // 256)
-        n, h = c1 - c0, c0 // 1024
+        h = c0 // 1024
+        cols = slice(c0, c1)
         wend = NT + NE * d if ask else NT
         lst = T["l%d" % d][:, c0 // 16:c1 // 16]
-        dep = [have[(d, h)]] + (["ad%d" % j for j, lv in enumerate(SENDS) if lv[0] < d] if ask else [])
-        xg, vg, pp = T["xg%d" % d], T["vg%d" % d], T["pp%d" % d]
+        dep = have(d, c0, c1) + (["ad%d" % j for j, lv in enumerate(SENDS) if lv[0] < d] if ask else [])
+        x, v, p = T["xg%d" % d][:, cols], T["vg%d" % d][:, cols], T["pp%d" % d][:, cols]
+        for c in range(c0 // 256, c1 // 256):
+            made[(d, c)] = "s" + nm
         if style == "a":
-            op("k" + nm, "V", "tg", n, dep + ["lk", "lq" + "ab"[h]], lambda e, x=xg[:, c0:c1], wend=wend, lst=lst, q=T.qs[:, c0:c1]:
+            op("k" + nm, "V", "c", dep + ["lk", "lq" + "ab"[h]], lambda e, x=x, wend=wend, lst=lst, q=T.qs[:, cols]:
                V.tensor_tensor(x, T.kw[:, 0:wend].indirect(lst), q, ALU.subtract))
-
-            def relu(e, x=xg[:, c0:c1], b=T.bs[:, d - 1:d]):
-                if e == "V":
-                    return V.tensor_scalar(x, x, b, 0.0, ALU.subtract, ALU.min)
-                return S.activation(x, x, ACT.Relu, bias=b, scale=-1.0)
-            op("r" + nm, "VS", "h", n, ["k" + nm, "lb"], relu)
-            op("s" + nm, "V", "tg", n, dep + ["r" + nm, "lv"], lambda e, x=xg[:, c0:c1], p=pp[:, c0:c1], wend=wend, lst=lst:
+            ts("r" + nm, x, x, T.bb[:, d - 1:d], 0.0, ALU.subtract, ALU.min, ["k" + nm, "bb"])
+            op("s" + nm, "V", "c", dep + ["r" + nm, "lv"], lambda e, x=x, p=p, wend=wend, lst=lst:
                V.tensor_tensor(p, T.vw[:, 0:wend].indirect(lst), x, ALU.mult))
-            for c in range(c0 // 256, c1 // 256):
-                made[(d, c)] = "s" + nm
-                minus[(d, c)] = "r" + nm in ORDER["V"].split()
-            continue
-        scale("v" + nm, vg[:, c0:c1], lambda wend=wend, lst=lst: T.vw[:, 0:wend].indirect(lst), n, TINY, None, dep + ["lv"], "g")
-        scale("k" + nm, xg[:, c0:c1], lambda wend=wend, lst=lst: T.kw[:, 0:wend].indirect(lst), n, -BIG, T.bx[:, d - 1:d],
-              dep + ["lk", "bx"], "g")
-        for a in range(c0, c1, 512):
-            z = min(a + 512, c1)
-            sn = "%d%d" % (d, a // 256)
-            bank = (T.xa, T.xb)[len(xq) % 2][:, 0:z - a]
+        else:
+            scale("v" + nm, v, lambda wend=wend, lst=lst: T.vw[:, 0:wend].indirect(lst), -TINY, None, dep + ["lv"])
+            scale("k" + nm, x, lambda wend=wend, lst=lst: T.kw[:, 0:wend].indirect(lst), -BIG, T.bx[:, d - 1:d], dep + ["lk", "bx"])
+            if style == "d":
+                for a in range(c0, c1, 512):
+                    sn, bank = "%d%d" % (d, a // 256), T["up%d" % (2 + len(xq) % 2)][:]
 
-            def xm(e, bank=bank, xg=xg, a=a, z=z):
-                P.matmul(bank, T.idx[:], T.qs[:, a:z], True, False)
-                return P.matmul(bank, T.idb[:], xg[:, a:z], False, True)
-            op("x" + sn, "P", "mm", 2 * (z - a), ["k" + nm, "ib", "ix", "lq" + "ab"[h]] + xq[-2:-1], xm)
-            op("s" + sn, "V", "f", z - a, ["x" + sn, "v" + nm], lambda e, bank=bank, v=vg[:, a:z], p=pp[:, a:z]:
-               V.tensor_tensor_scan(p, bank, v, 0.0, ALU.max, ALU.mult))
-            xq.append("s" + sn)
-            for c in range(a // 256, z // 256):
-                made[(d, c)] = "s" + sn
+                    def xm(e, bank=bank, k=T["xg%d" % d][:, a:a + 512], q=T.qs[:, a:a + 512]):
+                        P.matmul(bank, T.idx[:], q, True, False)
+                        return P.matmul(bank, T.idb[:], k, False, True)
+                    op("x" + sn, "P", "c", ["k" + nm, "ib", "ix", "lq" + "ab"[h]] + xq[-2:-1], xm)
+                    op("s" + sn, "V", "c", ["x" + sn, "v" + nm], lambda e, x=bank, v=T["vg%d" % d][:, a:a + 512], p=T["pp%d" % d][:, a:a + 512]:
+                       V.tensor_tensor_scan(p, x, v, 0.0, ALU.max, ALU.mult))
+                    xq.append("s" + sn)
+                    made[(d, a // 256)] = made[(d, a // 256 + 1)] = "s" + sn
+                continue
+            op("r" + nm, "G", "dma", ["k" + nm, "qa%d" % h], lambda e, x=x, q=T.qa[:, cols]: g.dma_start(x, q, accum_op=ALU.add),
+               sem="dx%d" % nadd)
+            nadd += 1
+            op("s" + nm, "V", "c", ["r" + nm, "v" + nm], lambda e, x=x, v=v, p=p: V.tensor_tensor_scan(p, x, v, 0.0, ALU.max, ALU.mult))
 
+    naccs = [3 + any(c0 // 512 == c and mode == "S" for c0, _, mode in FINALS) for c in range(4)]
+    seen = [0, 0, 0, 0]
     for d in range(1, ND + 1):
         for c in range(4):
             if d <= naccs[c]:
                 def acc(e, d=d, c=c):
                     seen[c] += 1
-                    return P.matmul(T["acc%d" % c][:], (T.idn if minus.get((d, 2 * c)) else T.idh)[:],
-                                    T["pp%d" % d][:, 512 * c:512 * c + 512], seen[c] == 1, seen[c] == naccs[c])
-                op("a%d%d" % (d, c), "P", "mm", 512,
-                   sorted(set([made[(d, 2 * c)], made[(d, 2 * c + 1)], "ih", "in"])) + (["c3e"] if c == 3 else []), acc)
-                accs[c].append("a%d%d" % (d, c))
+                    return P.matmul(T["acc%d" % c][:], T.idn[:], T["pp%d" % d][:, 512 * c:512 * c + 512], seen[c] == 1, seen[c] == naccs[c])
+                op("a%d%d" % (d, c), "P", "c", [made[(d, 2 * c)], made[(d, 2 * c + 1)], "in"] + (["c3e"] if c == 3 else []), acc)
     for j, (c0, c1, mode) in enumerate(FINALS):
         c = c0 // 512
         bank = T["acc%d" % c][:, c0 - 512 * c:c1 - 512 * c]
+        accs = ["a%d%d" % (d, c) for d in range(1, naccs[c] + 1)]
         if mode == "V":
-            op("f%d" % j, "V", "f", c1 - c0, accs[c] + sorted(set(made[(ND, x)] for x in range(c0 // 256, (c1 + 255) // 256))),
-               lambda e, bank=bank, c0=c0, c1=c1: V.tensor_tensor(T.ys[:, c0:c1], bank, T.pp4[:, c0:c1],
-                                                                  ALU.subtract if minus.get((ND, c0 // 256)) else ALU.add))
+            op("f%d" % j, "V", "c", accs + [made[(ND, x)] for x in range(c0 // 256, c1 // 256)],
+               lambda e, bank=bank, c0=c0, c1=c1: V.tensor_tensor(T.ys[:, c0:c1], bank, T.pp4[:, c0:c1], ALU.subtract))
         else:
-            scale("f%d" % j, T.ys[:, c0:c1], lambda bank=bank: bank, c1 - c0, 1.0, None, accs[c], "f")
-        load("st%d" % j, T.y[:, c0:c1], T.ys[:, c0:c1], 512 * (c1 - c0), ["f%d" % j])
+            scale("f%d" % j, T.ys[:, c0:c1], lambda bank=bank: bank, 1.0, None, accs)
+        load("st%d" % j, T.y[:, c0:c1], T.ys[:, c0:c1], ["f%d" % j])
     return ops
 
 
@@ -281,7 +288,7 @@ def rank_program(g, core, T, topo):
     for n, o in ops.items():
         if o["kind"] == "arr":
             tok[n] = o["tok"]
-    assert all(n in tok for n in ops)
+    assert all(n in tok for n in ops), [n for n in ops if n not in tok]
     for e, q in queue.items():
         waited = {}
         for n in order[e]:

@@ -6,6 +6,10 @@ ACT = ActivationFunctionType
 NT, NE, ND = 2048, 128, 4
 BIG = float(2 ** 50)
 TINY = 1.0 / BIG
+FINE = float(2 ** 20)
+ROUND = 1.5 * 2 ** 23
+TABLED = [[0, 1], [2]]
+QCUTS = [0, 1024, 2048]
 
 LIFTS = {1: [0, 1024, 2048], 2: [0, 1024, 2048], 3: [0, 1024, 2048]}
 UNITS = [(1, 0, 1024, "a"), (1, 1024, 2048, "e"), (2, 0, 1024, "e"), (3, 0, 1024, "a"), (4, 0, 1024, "e"), (2, 1024, 2048, "a"),
@@ -33,6 +37,30 @@ ORDER = {
     "G": "iz ic im id sx sd0 sd1 sd2 r14 r20 r40 r34",
 }
 
+UNITS = [(1, 0, 1024, "a"), (1, 1024, 2048, "e"), (2, 0, 1280, "e"), (3, 0, 1024, "a"), (4, 0, 1024, "e"), (2, 1280, 2048, "a"),
+         (3, 1024, 2048, "e"), (4, 1024, 1536, "a"), (4, 1536, 2048, "a")]
+FINALS = [(0, 512, "S"), (512, 1024, "S"), (1024, 1536, "S"), (1536, 1792, "V"), (1792, 2048, "V")]
+AFTER = {"lqa": ["lk"], "lqb": ["sd0"]}
+ORDER = {
+    "V": "z0 ca z1 k1 cw cf cm cl cb z2 d1 k3 d2 k2 d3 up w6 w0 w3 w7 w2 g1a xu sv0 c1b in bx c1a bb g2a c1e c2b g2e c2a sk1 sv1 c2e g3e k10 c3e c3b sv2 r10 k25 qa1 c3a r25 s10 s25 k44 k30 s20 r30 r44 s30 s44 s40 s14 k46 s34 r46 s46 f3 f4",
+    "S": "lp1 lup lv e0 e2 e1 w5 w4 w1 g1b sk0 g1e g2b qa0 g3b g3a sk2 k20 k14 v20 k40 k34 v40 v14 v34 f1 f0 f2",
+    "P": "m1b m1a m1e m2b m2a m2e m3e m3b m3a a10 a22 a11 a21 a42 a31 a41 a30 a20 a40 a12 a13 a32 a23 a33",
+    "Y": "lp0 lex lb lk lqa lqb st1 st0 st2 st3 st4",
+    "G": "iz im ic id sx sd0 sd1 sd2 r20 r14 r40 r34",
+}
+
+QCUTS = [0, 512, 1024, 1536, 2048]
+UNITS = [(1, 0, 1024, "a"), (1, 1024, 2048, "e"), (2, 0, 1024, "e"), (3, 0, 1024, "a"), (4, 0, 1024, "e"), (2, 1024, 2048, "a"),
+         (3, 1024, 2048, "e"), (4, 1024, 1536, "a"), (4, 1536, 2048, "a")]
+AFTER = {"lqa": ["lk"], "lqb": ["lk"]}
+ORDER = {
+    "V": "z0 ca z1 k1 cw cm k3 cl cf z2 d1 cb d2 k2 d3 up w7 w2 w3 w1 w6 g1a xu g1e in c1a qa0 c1e g2e c1b sk1 qa1 c2e sv1 g3e qa3 c2a qa2 c3e sv2 sk2 c2b k10 c3a k24 c3b r10 k44 k30 r44 s10 r24 r30 s24 s30 s20 s44 s40 k46 s14 s34 r46 s46 f3 f4",
+    "S": "lp1 lup lv e0 e2 e1 w0 w4 w5 bx g1b sv0 sk0 bb g2a g2b g3a g3b k14 k40 k20 k34 v40 v20 v14 v34 f1 f0 f2",
+    "P": "m1a m1e m1b m2e m2a m3e m2b m3a m3b a30 a11 a31 a23 a20 a21 a41 a42 a10 a40 a22 a12 a32 a33 a13",
+    "Y": "lp0 lex lb lk lqa lqb st1 st0 st2 st3 st4",
+    "G": "iz im ic id sx sd0 sd1 sd2 r14 r40 r20 r34",
+}
+
 SCRATCH = {
     "pc": ("sbuf", [128, 256], "int32"), "d1": ("sbuf", [128, 256], "int32"), "d2": ("sbuf", [128, 256], "int32"),
     "d3": ("sbuf", [128, 256], "bfloat16"), "pw": ("sbuf", [128, 2432], "bfloat16"),
@@ -47,6 +75,9 @@ SCRATCH = {
     "cb": ("sbuf", [128, 4], "float32"), "msk": ("sbuf", [128, 8], "float32"), "mskb": ("sbuf", [128, 8], "bfloat16"),
     "icol": ("sbuf", [128, 128], "float32"), "idia": ("sbuf", [128, 128], "float32"),
     "zz": ("sbuf", [128, 144], "bfloat16"), "idn": ("sbuf", [128, 128], "float16"),
+    "vp": ("sbuf", [128, 2432], "float32"), "vf1": ("sbuf", [128, 2048], "float32"), "vf2": ("sbuf", [128, 2048], "float32"),
+    "vf3": ("sbuf", [128, 2048], "float32"), "zf": ("sbuf", [128, 144], "float32"), "cy": ("sbuf", [128, 4], "float32"),
+    "one": ("sbuf", [128, 512], "bfloat16"), "rnd": ("sbuf", [128, 128], "bfloat16"), "idf": ("sbuf", [128, 128], "bfloat16"),
     "idb": ("sbuf", [128, 128], "bfloat16"), "idx": ("sbuf", [128, 128], "bfloat16"),
 }
 for _d in range(1, 5):
@@ -69,6 +100,7 @@ def build(g, core, T, topo):
     ops = {}
     V, S, P = g.vector, g.scalar, g.tensor
     dq = {"S": g.scalar, "Y": g.sync}
+    carried = [(u[0], u[1]) for u in UNITS if u[3] == "f"]
 
     def op(name, eng, kind, deps, fn, **kw):
         ops[name] = dict(eng=eng, kind=kind, deps=list(deps), fn=fn, **kw)
@@ -128,10 +160,8 @@ def build(g, core, T, topo):
         scale("ix", T.idx[:], lambda: T.idb[:], BIG, None, ["ib"])
     scale("bb", T.bb[:], lambda: T.bs[:], 1.0, None, ["lb"])
     scale("bx", T.bx[:], lambda: T.bs[:], BIG, None, ["lb"])
-    for h in range(2):
-        used = [c for u in UNITS if u[3] == "e" and u[1] // 1024 == h for c in u[1:3]]
-        if used:
-            scale("qa%d" % h, T.qa[:, min(used):max(used)], lambda a=min(used), z=max(used): T.qs[:, a:z], BIG, None, ["lq" + "ab"[h]])
+    for i, (a, z) in enumerate(zip(QCUTS, QCUTS[1:])):
+        scale("qa%d" % i, T.qa[:, a:z], lambda a=a, z=z: T.qs[:, a:z], BIG, None, ["lq" + "ab"[a // 1024]])
     win = ["w%d" % i for i in range(8)]
     if ask:
         ts("cl", T.cf[:, 2:3], odd, -0.125, 0.125, ALU.mult, ALU.add, ["ca"])
@@ -183,6 +213,8 @@ def build(g, core, T, topo):
 
     for lv, cuts in LIFTS.items():
         for i, (a, z) in enumerate(zip(cuts, cuts[1:])):
+            if (lv, a) in carried:
+                continue
             lift("%d%s" % (lv, "abcd"[i]), T["l%d" % lv][:, a // 16:z // 16], (z - a) // 16, T["ga%d" % lv], a, T["up%d" % i],
                  T["l%d" % (lv + 1)][:, a // 16:z // 16], have(lv, a, z))
 
@@ -207,6 +239,31 @@ def build(g, core, T, topo):
         for j in range(len(SENDS)):
             op("ad%d" % j, "", "arr", ["sd%d" % j], None, tok=("ad%d" % j, NENG))
 
+    if carried:
+        ts("if", T.idf[:], T.idia[:], 0.0, FINE, ALU.is_equal, ALU.mult, ["id"])
+        ts("y1", T.ia[:, 1:2], T.iz[:, 0:1], 15, None, ALU.bitwise_and, None, ["iz"])
+        ts("y2", T.cy[:, 0:1], T.ia[:, 1:2], 0.0, 1280 * TINY / FINE, ALU.is_equal, ALU.mult, ["y1"])
+        op("y3", "V", "c", [], lambda e: V.memset(T.zf[:], 0.0))
+        ts("y4", T.zf[:, 15:143:16], T.iz[:], 0.0, -BIG * FINE, ALU.is_equal, ALU.mult, ["y3", "iz"])
+        op("y5", "V", "c", [], lambda e: V.memset(T.one[:], 1.0))
+        op("y6", "V", "c", [], lambda e: V.memset(T.rnd[:], ROUND))
+
+        def table(nm, bank, a, z, deps):
+            def mm(e):
+                P.matmul(bank[:, 0:z - a], T.zz[:, 15:143], T.pw[:, a:z], True, False)
+                return P.matmul(bank[:, 0:z - a], T.idf[:], T.vw[:, a:z], False, True)
+            op("n" + nm, "P", "c", deps + ["z2", "if"], mm)
+            scale("t" + nm, T.vp[:, a:z], lambda: bank[:, 0:z - a], -TINY / FINE, T.cy[:, 0:1], ["n" + nm, "y2"])
+        for j in range(4):
+            table("%d" % j, (T.acc0, T.acc1, T.acc2, T.up2)[j], 512 * j, 512 * j + 512, ["w%d" % (2 * j), "w%d" % (2 * j + 1), "lv"])
+        if ask:
+            for j, lv in enumerate(TABLED):
+                table("e%d" % j, T.up3, NT + NE * lv[0], NT + NE * (lv[-1] + 1),
+                      ["e%d" % t for t in lv] + ["te%d" % (j - 1)] + ["ad%d" % i for i, s in enumerate(SENDS) if s[0] <= lv[-1]])
+        for c in range(4):
+            op("o%d" % c, "P", "c", ["y5", "y6", "c3e" if c == 3 else "t%d" % c],
+               lambda e, c=c: P.matmul(T["acc%d" % c][:], T.rnd[0:1, :], T.one[0:1, :], True, False))
+
     made, nadd, xq = {}, 0, []
     for d, c0, c1, style in UNITS:
         nm = "%d%d" % (d, c0 // 256)
@@ -225,7 +282,25 @@ def build(g, core, T, topo):
             op("s" + nm, "V", "c", dep + ["r" + nm, "lv"], lambda e, x=x, p=p, wend=wend, lst=lst:
                V.tensor_tensor(p, T.vw[:, 0:wend].indirect(lst), x, ALU.mult))
         else:
-            scale("v" + nm, v, lambda wend=wend, lst=lst: T.vw[:, 0:wend].indirect(lst), -TINY, None, dep + ["lv"])
+            vdone = "v" + nm
+            if style == "f":
+                vf, ln, bank, lc = T["vf%d" % d], "%d%s" % (d, "ab"[h]), T["up%d" % h], slice(64 * h, 64 * h + 64)
+                scale("v" + nm, vf[:, cols], lambda wend=wend, lst=lst: T.vp[:, 0:wend].indirect(lst), 1.0, None,
+                      have(d, c0, c1) + ["t%d" % j for j in range(4)] + ["te%d" % j for j, lv in enumerate(TABLED) if lv[0] < d])
+                op("u" + nm, "G", "dma", ["v" + nm], lambda e, a=v, b=vf[:, cols]: g.dma_start(a, b), sem="dx%d" % nadd)
+                nadd += 1
+                vdone = "u" + nm
+
+                def mm(e, vf=vf, bank=bank, c0=c0):
+                    for i in range(16):
+                        r = P.matmul(bank[:, 0:64], T.zf[:, 15 - i:143 - i], vf[:, c0 + i:c0 + 1024:16], i == 0, i == 15)
+                    return r
+                op("m" + ln, "P", "c", ["v" + nm, "y4"], mm)
+                ts("h" + ln, T.d1[:, lc], bank[:, 0:64], 1280.0, None, ALU.add, None, ["m" + ln, "d2"])
+                ts("i" + ln, T.d2[:, lc], T.d1[:, lc], 4095, None, ALU.bitwise_and, None, ["h" + ln, "d3"])
+                op("c" + ln, "V", "c", ["i" + ln], lambda e, o=T["l%d" % (d + 1)][:, lc], i=T.d2[:, lc]: V.tensor_copy(o, i))
+            else:
+                scale("v" + nm, v, lambda wend=wend, lst=lst: T.vw[:, 0:wend].indirect(lst), -TINY, None, dep + ["lv"])
             scale("k" + nm, x, lambda wend=wend, lst=lst: T.kw[:, 0:wend].indirect(lst), -BIG, T.bx[:, d - 1:d], dep + ["lk", "bx"])
             if style == "d":
                 for a in range(c0, c1, 512):
@@ -240,10 +315,10 @@ def build(g, core, T, topo):
                     xq.append("s" + sn)
                     made[(d, a // 256)] = made[(d, a // 256 + 1)] = "s" + sn
                 continue
-            op("r" + nm, "G", "dma", ["k" + nm, "qa%d" % h], lambda e, x=x, q=T.qa[:, cols]: g.dma_start(x, q, accum_op=ALU.add),
+            op("r" + nm, "G", "dma", ["k" + nm] + ["qa%d" % i for i in range(len(QCUTS) - 1) if QCUTS[i] < c1 and c0 < QCUTS[i + 1]], lambda e, x=x, q=T.qa[:, cols]: g.dma_start(x, q, accum_op=ALU.add),
                sem="dx%d" % nadd)
             nadd += 1
-            op("s" + nm, "V", "c", ["r" + nm, "v" + nm], lambda e, x=x, v=v, p=p: V.tensor_tensor_scan(p, x, v, 0.0, ALU.max, ALU.mult))
+            op("s" + nm, "V", "c", ["r" + nm, vdone], lambda e, x=x, v=v, p=p: V.tensor_tensor_scan(p, x, v, 0.0, ALU.max, ALU.mult))
 
     naccs = [3 + any(c0 // 512 == c and mode == "S" for c0, _, mode in FINALS) for c in range(4)]
     seen = [0, 0, 0, 0]
@@ -252,8 +327,9 @@ def build(g, core, T, topo):
             if d <= naccs[c]:
                 def acc(e, d=d, c=c):
                     seen[c] += 1
-                    return P.matmul(T["acc%d" % c][:], T.idn[:], T["pp%d" % d][:, 512 * c:512 * c + 512], seen[c] == 1, seen[c] == naccs[c])
-                op("a%d%d" % (d, c), "P", "c", [made[(d, 2 * c)], made[(d, 2 * c + 1)], "in"] + (["c3e"] if c == 3 else []), acc)
+                    return P.matmul(T["acc%d" % c][:], T.idn[:], T["pp%d" % d][:, 512 * c:512 * c + 512], seen[c] == 1 and not carried,
+                                    seen[c] == naccs[c])
+                op("a%d%d" % (d, c), "P", "c", [made[(d, 2 * c)], made[(d, 2 * c + 1)], "in", "o%d" % c] + (["c3e"] if c == 3 else []), acc)
     for j, (c0, c1, mode) in enumerate(FINALS):
         c = c0 // 512
         bank = T["acc%d" % c][:, c0 - 512 * c:c1 - 512 * c]
@@ -262,7 +338,7 @@ def build(g, core, T, topo):
             op("f%d" % j, "V", "c", accs + [made[(ND, x)] for x in range(c0 // 256, c1 // 256)],
                lambda e, bank=bank, c0=c0, c1=c1: V.tensor_tensor(T.ys[:, c0:c1], bank, T.pp4[:, c0:c1], ALU.subtract))
         else:
-            scale("f%d" % j, T.ys[:, c0:c1], lambda bank=bank: bank, 1.0, None, accs)
+            scale("f%d" % j, T.ys[:, c0:c1], lambda bank=bank: bank, 1.0, -ROUND if carried else None, accs)
         load("st%d" % j, T.y[:, c0:c1], T.ys[:, c0:c1], ["f%d" % j])
     return ops
 

from concourse.bass import DstId, RemoteDMATransfer
from concourse.mybir import AluOpType, ActivationFunctionType

ALU = AluOpType
ACT = ActivationFunctionType
NT, NE, ND = 2048, 128, 4
BIG = float(2 ** 50)
TINY = 1.0 / BIG
FINE = float(2 ** 20)
ROUND = 1.5 * 2 ** 23
TABLED = [[0, 1], [2]]
QCUTS = [0, 1024, 2048]

LIFTS = {1: [0, 1024, 2048], 2: [0, 1024, 2048], 3: [0, 1024, 2048]}
UNITS = [(1, 0, 1024, "a"), (1, 1024, 2048, "e"), (2, 0, 1024, "e"), (3, 0, 1024, "a"), (4, 0, 1024, "e"), (2, 1024, 2048, "a"),
         (3, 1024, 1536, "e"), (4, 1024, 1536, "a"), (3, 1536, 2048, "e"), (4, 1536, 2048, "a")]
FINALS = [(0, 512, "S"), (512, 1024, "S"), (1024, 1536, "S"), (1536, 2048, "V")]
SENDS = [[0], [1], [2, 3]]
NENG = 8
AFTER = {"lqa": ["sx"], "lqb": ["sd0"]}
ORDER = {
    "V": "z0 ca cl k1 k2 cf z1 cm k3 cb cw d1 d2 d3 w2 w7 up w6 w0 w3 z2 g1a in xu sv0 c1b g1e c1a g2a c1e qa0 c2a c2e g3e sk1 c2b c3e k10 qa1 r10 k24 c3b r24 c3a k30 k44 s10 s24 r44 r30 s20 s30 k46 s40 s14 s44 s34 r46 s36 s46 f3",
    "S": "lp1 lup lv e1 e2 e0 w1 w5 w4 g1b sk0 g2b bb g2e sv1 bx g3a sk2 sv2 g3b k14 k20 k40 v20 k36 k34 v40 v14 v34 v36 f1 f0 f2",
    "P": "m1b m1a m1e m2a m2e m2b m3e m3a m3b a30 a21 a20 a31 a11 a41 a40 a10 a12 a42 a22 a32 a23 a13 a33",
    "Y": "lp0 lex lb lk lqa lqb st1 st0 st2 st3",
    "G": "iz im id ic sx sd0 sd1 sd2 r14 r20 r40 r34 r36",
}

UNITS = [(1, 0, 1024, "a"), (1, 1024, 2048, "e"), (2, 0, 1024, "e"), (3, 0, 1024, "a"), (4, 0, 1024, "e"), (2, 1024, 2048, "a"),
         (3, 1024, 2048, "e"), (4, 1024, 1536, "a"), (4, 1536, 1792, "a"), (4, 1792, 2048, "a")]
FINALS = [(0, 512, "S"), (512, 1024, "S"), (1024, 1536, "S"), (1536, 1792, "V"), (1792, 2048, "V")]
ORDER = {
    "V": "z0 ca cl cf cb cm k1 k2 z1 k3 d1 d2 d3 w2 up w5 w1 w7 w6 in cw z2 g1a xu sv0 c1b c1a g2a c1e c2b c2e g3e qa0 c2a sv1 c3e k10 c3b r10 qa1 c3a s10 k24 k30 r24 k44 r30 s24 s30 s20 s40 k46 s14 r44 s44 s34 k47 r47 s47 f4 r46 s46 f3",
    "S": "lp1 lup lv e1 e2 e0 w3 w4 w0 bb g1b sk0 g1e bx g2b g2e sk1 g3b g3a sk2 sv2 k14 k20 k40 k34 v40 v20 v14 v34 f0 f1 f2 st2",
    "P": "m1b m1a m1e m2b m2e m2a m3e m3b m3a a10 a22 a30 a21 a11 a23 a31 a20 a40 a13 a41 a42 a12 a32 a33",
    "Y": "lp0 lex lb lk lqa lqb st0 st1 st4 st3",
    "G": "iz ic im id sx sd0 sd1 sd2 r14 r20 r40 r34",
}

UNITS = [(1, 0, 1024, "a"), (1, 1024, 2048, "e"), (2, 0, 1280, "e"), (3, 0, 1024, "a"), (4, 0, 1024, "e"), (2, 1280, 2048, "a"),
         (3, 1024, 2048, "e"), (4, 1024, 1536, "a"), (4, 1536, 2048, "a")]
FINALS = [(0, 512, "S"), (512, 1024, "S"), (1024, 1536, "S"), (1536, 1792, "V"), (1792, 2048, "V")]
AFTER = {"lqa": ["lk"], "lqb": ["sd0"]}
ORDER = {
    "V": "z0 ca z1 k1 cw cf cm cl cb z2 d1 k3 d2 k2 d3 up w6 w0 w3 w7 w2 g1a xu sv0 c1b in bx c1a bb g2a c1e c2b g2e c2a sk1 sv1 c2e g3e k10 c3e c3b sv2 r10 k25 qa1 c3a r25 s10 s25 k44 k30 s20 r30 r44 s30 s44 s40 s14 k46 s34 r46 s46 f3 f4",
    "S": "lp1 lup lv e0 e2 e1 w5 w4 w1 g1b sk0 g1e g2b qa0 g3b g3a sk2 k20 k14 v20 k40 k34 v40 v14 v34 f1 f0 f2",
    "P": "m1b m1a m1e m2b m2a m2e m3e m3b m3a a10 a22 a11 a21 a42 a31 a41 a30 a20 a40 a12 a13 a32 a23 a33",
    "Y": "lp0 lex lb lk lqa lqb st1 st0 st2 st3 st4",
    "G": "iz im ic id sx sd0 sd1 sd2 r20 r14 r40 r34",
}

QCUTS = [0, 512, 1024, 1536, 2048]
UNITS = [(1, 0, 1024, "a"), (1, 1024, 2048, "e"), (2, 0, 1024, "e"), (3, 0, 1024, "a"), (4, 0, 1024, "e"), (2, 1024, 2048, "a"),
         (3, 1024, 2048, "e"), (4, 1024, 1536, "a"), (4, 1536, 2048, "a")]
AFTER = {"lqa": ["lk"], "lqb": ["lk"]}
ORDER = {
    "V": "z0 ca z1 k1 cw cm k3 cl cf z2 d1 cb d2 k2 d3 up w7 w2 w3 w1 w6 g1a xu g1e in c1a qa0 c1e g2e c1b sk1 qa1 c2e sv1 g3e qa3 c2a qa2 c3e sv2 sk2 c2b k10 c3a k24 c3b r10 k44 k30 r44 s10 r24 r30 s24 s30 s20 s44 s40 k46 s14 s34 r46 s46 f3 f4",
    "S": "lp1 lup lv e0 e2 e1 w0 w4 w5 bx g1b sv0 sk0 bb g2a g2b g3a g3b k14 k40 k20 k34 v40 v20 v14 v34 f1 f0 f2",
    "P": "m1a m1e m1b m2e m2a m3e m2b m3a m3b a30 a11 a31 a23 a20 a21 a41 a42 a10 a40 a22 a12 a32 a33 a13",
    "Y": "lp0 lex lb lk lqa lqb st1 st0 st2 st3 st4",
    "G": "iz im ic id sx sd0 sd1 sd2 r14 r40 r20 r34",
}

SCRATCH = {
    "pc": ("sbuf", [128, 256], "int32"), "d1": ("sbuf", [128, 256], "int32"), "d2": ("sbuf", [128, 256], "int32"),
    "d3": ("sbuf", [128, 256], "bfloat16"), "pw": ("sbuf", [128, 2432], "bfloat16"),
    "upi": ("sbuf", [128, 128], "int32"), "exi": ("sbuf", [128, 8], "int32"), "exr": ("sbuf", [128, 8], "int32"),
    "el": ("sbuf", [128, 32], "uint16"), "ga4": ("sbuf", [128, 384], "bfloat16"),
    "kw": ("sbuf", [128, 2560], "bfloat16"), "vw": ("sbuf", [128, 2560], "bfloat16"),
    "qs": ("sbuf", [128, 2048], "bfloat16"), "qa": ("sbuf", [128, 2048], "bfloat16"),
    "bs": ("sbuf", [128, 4], "float32"), "bx": ("sbuf", [128, 4], "float32"), "bb": ("sbuf", [128, 4], "bfloat16"),
    "ys": ("sbuf", [128, 2048], "float32"), "sk": ("sbuf", [128, 512], "bfloat16"), "sv": ("sbuf", [128, 512], "bfloat16"),
    "im": ("sbuf", [128, 8], "int32"), "iz": ("sbuf", [128, 8], "int32"), "im2": ("sbuf", [128, 8], "int32"),
    "iz2": ("sbuf", [128, 8], "int32"), "ia": ("sbuf", [128, 4], "int32"), "cf": ("sbuf", [128, 4], "float32"),
    "cb": ("sbuf", [128, 4], "float32"), "msk": ("sbuf", [128, 8], "float32"), "mskb": ("sbuf", [128, 8], "bfloat16"),
    "icol": ("sbuf", [128, 128], "float32"), "idia": ("sbuf", [128, 128], "float32"),
    "zz": ("sbuf", [128, 144], "bfloat16"), "idn": ("sbuf", [128, 128], "float16"),
    "vp": ("sbuf", [128, 2432], "float32"), "vf1": ("sbuf", [128, 2048], "float32"), "vf2": ("sbuf", [128, 2048], "float32"),
    "vf3": ("sbuf", [128, 2048], "float32"), "zf": ("sbuf", [128, 144], "float32"), "cy": ("sbuf", [128, 4], "float32"),
    "one": ("sbuf", [128, 512], "bfloat16"), "rnd": ("sbuf", [128, 128], "bfloat16"), "idf": ("sbuf", [128, 128], "bfloat16"),
    "idb": ("sbuf", [128, 128], "bfloat16"), "idx": ("sbuf", [128, 128], "bfloat16"),
}
for _d in range(1, 5):
    SCRATCH["l%d" % _d] = ("sbuf", [128, 128], "uint16")
    SCRATCH["xg%d" % _d] = ("sbuf", [128, 2048], "bfloat16")
    SCRATCH["vg%d" % _d] = ("sbuf", [128, 2048], "bfloat16")
    SCRATCH["pp%d" % _d] = ("sbuf", [128, 2048], "float16")
    SCRATCH["acc%d" % (_d - 1)] = ("psum", [128, 512], "float32")
    SCRATCH["up%d" % (_d - 1)] = ("psum", [128, 512], "float32")
    if _d < 4:
        SCRATCH["ga%d" % _d] = ("sbuf", [128, 2048], "bfloat16")

SEMAPHORES = (["cV", "cS", "cP", "cG", "lex", "lp0", "lp1", "lup", "lb", "lk", "lv", "lqa", "lqb", "sx", "ax"]
              + ["%s%d" % (n, i) for n in ("sd", "ad", "st") for i in range(8)] + ["dx%d" % i for i in range(16)])


def build(g, core, T, topo):
    rank = T.rank_of(core)
    serve, ask = rank < len(T.cores) - 1, rank > 0
    ops = {}
    V, S, P = g.vector, g.scalar, g.tensor
    dq = {"S": g.scalar, "Y": g.sync}
    carried = [(u[0], u[1]) for u in UNITS if u[3] == "f"]

    def op(name, eng, kind, deps, fn, **kw):
        ops[name] = dict(eng=eng, kind=kind, deps=list(deps), fn=fn, **kw)

    def load(name, out, in_, deps=()):
        op(name, "YS", "dma", list(deps) + AFTER.get(name, []), lambda e: dq[e].dma_start(out, in_), sem=name)

    def scale(name, out, in_, s1, s2, deps, narrow=None):
        def fn(e):
            if e == "V":
                if narrow is not None:
                    return V.tensor_scalar(out, in_(), narrow, None, ALU.mult)
                if s2 is None:
                    if isinstance(s1, float) and s1 == 1.0:
                        return V.tensor_copy(out, in_())
                    return V.tensor_scalar(out, in_(), s1, None, ALU.mult)
                return V.tensor_scalar(out, in_(), s1, s2, ALU.mult, ALU.add)
            if s2 is None:
                return S.activation(out, in_(), ACT.Identity, scale=s1)
            return S.activation(out, in_(), ACT.Identity, bias=s2, scale=s1)
        op(name, "VS", "c", deps, fn)

    def ts(name, out, in0, s1, s2, o0, o1, deps):
        if o1 is None:
            op(name, "V", "c", deps, lambda e: V.tensor_scalar(out, in0, s1, None, o0))
        else:
            op(name, "V", "c", deps, lambda e: V.tensor_scalar(out, in0, s1, s2, o0, o1))

    if ask:
        load("lex", T.exi[:], T.ex[:])
    load("lp0", T.pc[0:128:2, :], T.par[:])
    load("lp1", T.pc[1:128:2, :], T.par[:])
    load("lup", T.upi[:], T.up[:])
    load("lb", T.bs[:], T.b[:])
    load("lk", T.kw[:, 0:NT], T.k[:])
    load("lv", T.vw[:, 0:NT], T.v[:])
    load("lqa", T.qs[:, 0:1024], T.q[:, 0:1024])
    load("lqb", T.qs[:, 1024:2048], T.q[:, 1024:2048])

    op("iz", "G", "c", [], lambda e: g.iota(T.iz[:], [[-16, 8]], 0, 1))
    op("im", "G", "c", [], lambda e: g.iota(T.im[:], [[-2, 8]], 16, 1))
    op("ic", "G", "c", [], lambda e: g.iota(T.icol[:], [[1, 128]], 0, 0, allow_small_or_imprecise_dtypes=True))
    op("id", "G", "c", [], lambda e: g.iota(T.idia[:], [[1, 128]], 0, -1, allow_small_or_imprecise_dtypes=True))
    odd = T.ia[:, 0:1]
    ts("ca", odd, T.iz[:, 0:1], 1, None, ALU.bitwise_and, None, ["iz"])
    ts("cm", T.cf[:, 0:1], odd, -127.0, 128.0, ALU.mult, ALU.add, ["ca"])
    ts("cw", T.cf[:, 1:2], odd, 127.0, 1.0, ALU.mult, ALU.add, ["ca"])
    ts("k1", T.im2[:], T.im[:], 14, None, ALU.bitwise_and, None, ["im"])
    ts("k2", T.msk[:], T.im2[:], 0.0, None, ALU.is_equal, None, ["k1"])
    ts("k3", T.mskb[:], T.im2[:], 0.0, None, ALU.is_equal, None, ["k1"])
    op("z0", "V", "c", [], lambda e: V.memset(T.zz[:], 0.0))
    ts("z1", T.iz2[:], T.iz[:], 4, None, ALU.arith_shift_right, None, ["iz"])
    ts("z2", T.zz[:, 15:143:16], T.iz2[:], 0.0, T.cf[:, 1:2], ALU.is_equal, ALU.mult, ["z0", "z1", "cw"])
    ts("in", T.idn[:], T.idia[:], 0.0, -1.0, ALU.is_equal, ALU.mult, ["id"])
    if any(u[3] == "d" for u in UNITS):
        ts("ib", T.idb[:], T.idia[:], 0.0, None, ALU.is_equal, None, ["id"])
        scale("ix", T.idx[:], lambda: T.idb[:], BIG, None, ["ib"])
    scale("bb", T.bb[:], lambda: T.bs[:], 1.0, None, ["lb"])
    scale("bx", T.bx[:], lambda: T.bs[:], BIG, None, ["lb"])
    for i, (a, z) in enumerate(zip(QCUTS, QCUTS[1:])):
        scale("qa%d" % i, T.qa[:, a:z], lambda a=a, z=z: T.qs[:, a:z], BIG, None, ["lq" + "ab"[a // 1024]])
    win = ["w%d" % i for i in range(8)]
    if ask:
        ts("cl", T.cf[:, 2:3], odd, -0.125, 0.125, ALU.mult, ALU.add, ["ca"])
        ts("cf", T.cf[:, 3:4], odd, 0.125, None, ALU.mult, None, ["ca"])
        ts("cb", T.cb[:, 0:3], T.icol[:, 17:20], T.cf[:, 3:4], None, ALU.mult, None, ["cf", "ic"])
        for t in range(3):
            scale("e%d" % t, T.pw[:, NT + NE * t:NT + NE * (t + 1)], lambda: T.icol[:], T.cf[:, 2:3], T.cb[:, t:t + 1], ["cl", "cb", "ic"])
            win.append("e%d" % t)
    pend = NT + 3 * NE if ask else NT

    ts("d1", T.d1[:], T.pc[:], T.cf[:, 0:1], None, ALU.mult, None, ["lp0", "lp1", "cm"])
    ts("d2", T.d2[:], T.d1[:], 7, 127, ALU.logical_shift_right, ALU.bitwise_and, ["d1"])
    op("d3", "V", "c", ["d2"], lambda e: V.tensor_copy(T.d3[:], T.d2[:]))
    for i in range(8):
        scale("w%d" % i, T.pw[:, 256 * i:256 * (i + 1)], lambda: T.d3[:], T.msk[:, i:i + 1], None, ["d3", "k2", "k3"], T.mskb[:, i:i + 1])
    op("up", "V", "c", ["lup"], lambda e: V.tensor_copy(T.l1[:], T.upi[:]))

    def dst(r):
        rid, pid, _ = topo.addr(T.cores[r])
        return rid, pid, topo.engines(core, T.cores[r])[:NENG]

    def bits(es):
        return sum(1 << x for x in es)

    xd = ["xu", "c1e", "c2e", "c3e"]
    if ask:
        rid, pid, es = dst(rank - 1)
        op("sx", "G", "rem", ["lex"], lambda e: g.remote_dma(T.exr[:], T.exi[:], T.sem.ax, T.sem.sx, pid, rid, bits(es)),
           tok=("sx", len(es)))
    if serve:
        op("ax", "", "arr", ["sx"], None, tok=("ax", NENG))
        op("xu", "V", "c", ["ax"], lambda e: V.tensor_copy(T.el[:, 0:8], T.exr[:]))

    def lift(name, lst, n, ga, base, bank, out, deps):
        scale("g" + name, ga[:, base:base + 16 * n], lambda: T.pw[:, 0:pend].indirect(lst), 1.0, None, win + deps)

        def mm(e):
            for i in range(16):
                r = P.matmul(bank[:, 0:n], T.zz[:, 15 - i:143 - i], ga[:, base + i:base + 16 * n:16], i == 0, i == 15)
            return r
        op("m" + name, "P", "c", ["g" + name, "z2", "c%d%s" % (int(name[0]) - 1, name[1])], mm)
        op("c" + name, "V", "c", ["m" + name], lambda e: V.tensor_copy(out, bank[:, 0:n]))

    def have(d, a, z):
        if d == 1:
            return ["up"]
        cuts = LIFTS[d - 1]
        return ["c%d%s" % (d - 1, "abcd"[i]) for i in range(len(cuts) - 1) if cuts[i] < z and a < cuts[i + 1]]

    for lv, cuts in LIFTS.items():
        for i, (a, z) in enumerate(zip(cuts, cuts[1:])):
            if (lv, a) in carried:
                continue
            lift("%d%s" % (lv, "abcd"[i]), T["l%d" % lv][:, a // 16:z // 16], (z - a) // 16, T["ga%d" % lv], a, T["up%d" % i],
                 T["l%d" % (lv + 1)][:, a // 16:z // 16], have(lv, a, z))

    if serve:
        for t in range(1, ND):
            lift("%de" % t, T.el[:, 8 * t - 8:8 * t], 8, T.ga4, NE * (t - 1), T.acc3, T.el[:, 8 * t:8 * t + 8], [xd[t - 1]])
        rid2, pid2, es2 = dst(rank + 1)
        half = len(es2) // 2
        for j, lv in enumerate(SENDS):
            a, z = NE * lv[0], NE * (lv[-1] + 1)
            lst = T.el[:, a // 16:z // 16]
            scale("sk%d" % j, T.sk[:, a:z], lambda lst=lst: T.kw[:, 0:NT].indirect(lst), 1.0, None, ["lk"] + [xd[t] for t in lv])
            scale("sv%d" % j, T.sv[:, a:z], lambda lst=lst: T.vw[:, 0:NT].indirect(lst), 1.0, None, ["lv"] + [xd[t] for t in lv])

            def send(e, j=j, a=a, z=z):
                return g.remote_dma_fused([
                    RemoteDMATransfer(dst_ids=[DstId(rid=rid2, pnc=pid2)], dma_engine_mask=bits(m), remote_sem=T.sem["ad%d" % j],
                                      src=s[:, a:z], dst=w[:, NT + a:NT + z])
                    for s, w, m in ((T.sk, T.kw, es2[:half]), (T.sv, T.vw, es2[half:]))], local_sem=T.sem["sd%d" % j])
            op("sd%d" % j, "G", "rem", ["sk%d" % j, "sv%d" % j], send, tok=("sd%d" % j, len(es2)))
    if ask:
        for j in range(len(SENDS)):
            op("ad%d" % j, "", "arr", ["sd%d" % j], None, tok=("ad%d" % j, NENG))

    if carried:
        ts("if", T.idf[:], T.idia[:], 0.0, FINE, ALU.is_equal, ALU.mult, ["id"])
        ts("y1", T.ia[:, 1:2], T.iz[:, 0:1], 15, None, ALU.bitwise_and, None, ["iz"])
        ts("y2", T.cy[:, 0:1], T.ia[:, 1:2], 0.0, 1280 * TINY / FINE, ALU.is_equal, ALU.mult, ["y1"])
        op("y3", "V", "c", [], lambda e: V.memset(T.zf[:], 0.0))
        ts("y4", T.zf[:, 15:143:16], T.iz[:], 0.0, -BIG * FINE, ALU.is_equal, ALU.mult, ["y3", "iz"])
        op("y5", "V", "c", [], lambda e: V.memset(T.one[:], 1.0))
        op("y6", "V", "c", [], lambda e: V.memset(T.rnd[:], ROUND))

        def table(nm, bank, a, z, deps):
            def mm(e):
                P.matmul(bank[:, 0:z - a], T.zz[:, 15:143], T.pw[:, a:z], True, False)
                return P.matmul(bank[:, 0:z - a], T.idf[:], T.vw[:, a:z], False, True)
            op("n" + nm, "P", "c", deps + ["z2", "if"], mm)
            scale("t" + nm, T.vp[:, a:z], lambda: bank[:, 0:z - a], -TINY / FINE, T.cy[:, 0:1], ["n" + nm, "y2"])
        for j in range(4):
            table("%d" % j, (T.acc0, T.acc1, T.acc2, T.up2)[j], 512 * j, 512 * j + 512, ["w%d" % (2 * j), "w%d" % (2 * j + 1), "lv"])
        if ask:
            for j, lv in enumerate(TABLED):
                table("e%d" % j, T.up3, NT + NE * lv[0], NT + NE * (lv[-1] + 1),
                      ["e%d" % t for t in lv] + ["te%d" % (j - 1)] + ["ad%d" % i for i, s in enumerate(SENDS) if s[0] <= lv[-1]])
        for c in range(4):
            op("o%d" % c, "P", "c", ["y5", "y6", "c3e" if c == 3 else "t%d" % c],
               lambda e, c=c: P.matmul(T["acc%d" % c][:], T.rnd[0:1, :], T.one[0:1, :], True, False))

    made, nadd, xq = {}, 0, []
    for d, c0, c1, style in UNITS:
        nm = "%d%d" % (d, c0 // 256)
        h = c0 // 1024
        cols = slice(c0, c1)
        wend = NT + NE * d if ask else NT
        lst = T["l%d" % d][:, c0 // 16:c1 // 16]
        dep = have(d, c0, c1) + (["ad%d" % j for j, lv in enumerate(SENDS) if lv[0] < d] if ask else [])
        x, v, p = T["xg%d" % d][:, cols], T["vg%d" % d][:, cols], T["pp%d" % d][:, cols]
        for c in range(c0 // 256, c1 // 256):
            made[(d, c)] = "s" + nm
        if style == "a":
            op("k" + nm, "V", "c", dep + ["lk", "lq" + "ab"[h]], lambda e, x=x, wend=wend, lst=lst, q=T.qs[:, cols]:
               V.tensor_tensor(x, T.kw[:, 0:wend].indirect(lst), q, ALU.subtract))
            ts("r" + nm, x, x, T.bb[:, d - 1:d], 0.0, ALU.subtract, ALU.min, ["k" + nm, "bb"])
            op("s" + nm, "V", "c", dep + ["r" + nm, "lv"], lambda e, x=x, p=p, wend=wend, lst=lst:
               V.tensor_tensor(p, T.vw[:, 0:wend].indirect(lst), x, ALU.mult))
        else:
            vdone = "v" + nm
            if style == "f":
                vf, ln, bank, lc = T["vf%d" % d], "%d%s" % (d, "ab"[h]), T["up%d" % h], slice(64 * h, 64 * h + 64)
                scale("v" + nm, vf[:, cols], lambda wend=wend, lst=lst: T.vp[:, 0:wend].indirect(lst), 1.0, None,
                      have(d, c0, c1) + ["t%d" % j for j in range(4)] + ["te%d" % j for j, lv in enumerate(TABLED) if lv[0] < d])
                op("u" + nm, "G", "dma", ["v" + nm], lambda e, a=v, b=vf[:, cols]: g.dma_start(a, b), sem="dx%d" % nadd)
                nadd += 1
                vdone = "u" + nm

                def mm(e, vf=vf, bank=bank, c0=c0):
                    for i in range(16):
                        r = P.matmul(bank[:, 0:64], T.zf[:, 15 - i:143 - i], vf[:, c0 + i:c0 + 1024:16], i == 0, i == 15)
                    return r
                op("m" + ln, "P", "c", ["v" + nm, "y4"], mm)
                ts("h" + ln, T.d1[:, lc], bank[:, 0:64], 1280.0, None, ALU.add, None, ["m" + ln, "d2"])
                ts("i" + ln, T.d2[:, lc], T.d1[:, lc], 4095, None, ALU.bitwise_and, None, ["h" + ln, "d3"])
                op("c" + ln, "V", "c", ["i" + ln], lambda e, o=T["l%d" % (d + 1)][:, lc], i=T.d2[:, lc]: V.tensor_copy(o, i))
            else:
                scale("v" + nm, v, lambda wend=wend, lst=lst: T.vw[:, 0:wend].indirect(lst), -TINY, None, dep + ["lv"])
            scale("k" + nm, x, lambda wend=wend, lst=lst: T.kw[:, 0:wend].indirect(lst), -BIG, T.bx[:, d - 1:d], dep + ["lk", "bx"])
            if style == "d":
                for a in range(c0, c1, 512):
                    sn, bank = "%d%d" % (d, a // 256), T["up%d" % (2 + len(xq) % 2)][:]

                    def xm(e, bank=bank, k=T["xg%d" % d][:, a:a + 512], q=T.qs[:, a:a + 512]):
                        P.matmul(bank, T.idx[:], q, True, False)
                        return P.matmul(bank, T.idb[:], k, False, True)
                    op("x" + sn, "P", "c", ["k" + nm, "ib", "ix", "lq" + "ab"[h]] + xq[-2:-1], xm)
                    op("s" + sn, "V", "c", ["x" + sn, "v" + nm], lambda e, x=bank, v=T["vg%d" % d][:, a:a + 512], p=T["pp%d" % d][:, a:a + 512]:
                       V.tensor_tensor_scan(p, x, v, 0.0, ALU.max, ALU.mult))
                    xq.append("s" + sn)
                    made[(d, a // 256)] = made[(d, a // 256 + 1)] = "s" + sn
                continue
            op("r" + nm, "G", "dma", ["k" + nm] + ["qa%d" % i for i in range(len(QCUTS) - 1) if QCUTS[i] < c1 and c0 < QCUTS[i + 1]], lambda e, x=x, q=T.qa[:, cols]: g.dma_start(x, q, accum_op=ALU.add),
               sem="dx%d" % nadd)
            nadd += 1
            op("s" + nm, "V", "c", ["r" + nm, vdone], lambda e, x=x, v=v, p=p: V.tensor_tensor_scan(p, x, v, 0.0, ALU.max, ALU.mult))

    naccs = [3 + any(c0 // 512 == c and mode == "S" for c0, _, mode in FINALS) for c in range(4)]
    seen = [0, 0, 0, 0]
    for d in range(1, ND + 1):
        for c in range(4):
            if d <= naccs[c]:
                def acc(e, d=d, c=c):
                    seen[c] += 1
                    return P.matmul(T["acc%d" % c][:], T.idn[:], T["pp%d" % d][:, 512 * c:512 * c + 512], seen[c] == 1 and not carried,
                                    seen[c] == naccs[c])
                op("a%d%d" % (d, c), "P", "c", [made[(d, 2 * c)], made[(d, 2 * c + 1)], "in", "o%d" % c] + (["c3e"] if c == 3 else []), acc)
    for j, (c0, c1, mode) in enumerate(FINALS):
        c = c0 // 512
        bank = T["acc%d" % c][:, c0 - 512 * c:c1 - 512 * c]
        accs = ["a%d%d" % (d, c) for d in range(1, naccs[c] + 1)]
        if mode == "V":
            op("f%d" % j, "V", "c", accs + [made[(ND, x)] for x in range(c0 // 256, c1 // 256)],
               lambda e, bank=bank, c0=c0, c1=c1: V.tensor_tensor(T.ys[:, c0:c1], bank, T.pp4[:, c0:c1], ALU.subtract))
        else:
            scale("f%d" % j, T.ys[:, c0:c1], lambda bank=bank: bank, 1.0, -ROUND if carried else None, accs)
        load("st%d" % j, T.y[:, c0:c1], T.ys[:, c0:c1], ["f%d" % j])
    return ops


def rank_program(g, core, T, topo):
    if T.rank_of(core) is None:
        return
    ops = build(g, core, T, topo)
    queue = {"V": g.vector, "S": g.scalar, "P": g.tensor, "Y": g.sync, "G": g}
    order = {e: [n for n in ORDER[e].split() if n in ops] for e in queue}
    tok, count, ends = {}, {}, []
    for e in queue:
        for n in order[e]:
            o = ops[n]
            if o["kind"] == "dma":
                tok[n] = (o["sem"], 16)
            elif o["kind"] == "rem":
                tok[n] = o["tok"]
                ends.append(tok[n])
            else:
                count[e] = count.get(e, 0) + 1
                tok[n] = ("c" + e, count[e])
    for n, o in ops.items():
        if o["kind"] == "arr":
            tok[n] = o["tok"]
    assert all(n in tok for n in ops), [n for n in ops if n not in tok]
    for e, q in queue.items():
        waited = {}
        for n in order[e]:
            o = ops[n]
            need = {}
            for d in o["deps"]:
                if d in tok:
                    s, val = tok[d]
                    need[s] = max(need.get(s, 0), val)
            for s, val in need.items():
                if waited.get(s, 0) < val:
                    q.wait_ge(T.sem[s], val)
                    waited[s] = val
            ins = o["fn"](e)
            if o["kind"] != "rem":
                ins.then_inc(T.sem[tok[n][0]], 16 if o["kind"] == "dma" else 1)
        if e == "Y":
            for j in range(len(FINALS)):
                q.wait_ge(T.sem["st%d" % j], 16)
        if e == "G":
            for s, val in ends + [("c" + x, count[x]) for x in count]:
                if waited.get(s, 0) < val:
                    q.wait_ge(T.sem[s], val)
